import numpy as np
import ml_dtypes


def mxq(x, axis, fmt="e4m3"):
    dtype, down = {"e4m3": (ml_dtypes.float8_e4m3fn, 7), "e5m2": (ml_dtypes.float8_e5m2, 14)}[fmt]
    v = np.moveaxis(np.asarray(x, np.float32).astype(ml_dtypes.bfloat16).astype(np.float64), axis, -1)
    blocks = v.reshape(v.shape[:-1] + (-1, 32))
    amax = np.abs(blocks).max(-1, keepdims=True)
    byte = np.maximum(np.where(amax > 0, np.frexp(amax)[1] - 1 + 127, 0) - down, 1)
    scale = np.exp2(byte - 127.0)
    codes = (blocks / scale).astype(np.float32).astype(dtype).astype(np.float64)
    return np.moveaxis((codes * scale).reshape(v.shape), -1, axis)


WIDE = False


def mx_kscale(k):
    if not WIDE:
        return np.ones(k)
    levels = np.array([10, -10, 5, -5, 0])
    if k % 512:
        return np.exp2(np.random.permutation(np.resize(levels, k // 32))).repeat(32)
    a = np.empty((k // 512, 16))
    for p in range(k // 512):
        a[p, :8] = np.random.permutation(np.resize(levels, 8))
        for g in range(8):
            far = levels[np.abs(levels - a[p, g]) >= 10]
            a[p, g + 8] = far[np.random.randint(len(far))]
    return np.exp2(a.ravel()).repeat(32)


def f64(x):
    return np.asarray(x).astype(np.float64)


def striped(idx):
    return np.tile(idx.reshape(-1, 16).T, (8, 1)).astype(np.uint16)


def unstriped(offs):
    return offs[:16].T.reshape(-1).astype(np.int64)


def striped8(idx):
    return np.concatenate([x.reshape(-1, 16).T for x in idx]).astype(np.uint16)


def runs(offs, k):
    lists = np.stack([offs[16 * r : 16 * r + 16].T.reshape(-1) for r in range(8)]).astype(np.int64)
    return lists[np.arange(k) % 512 // 64]


def pack_weight(w):
    k, n = w.shape
    w = f64(np.asarray(w, np.float32).astype(ml_dtypes.bfloat16)).reshape(k // 32, 32, n)
    amax = np.abs(w).max(1)
    byte = np.clip(np.where(amax > 0, np.frexp(amax)[1] - 1 + 127 - 7, 1), 1, 254)
    scaled = (w * np.exp2(127.0 - byte)[:, None, :]).reshape(k, n).astype(np.float32)
    words = np.ascontiguousarray(scaled.reshape(k // 512, 128, 4, n).transpose(0, 1, 3, 2)).astype(ml_dtypes.float8_e4m3fn).view(np.uint8)
    return words, np.ascontiguousarray(byte.astype(np.uint8).reshape(k // 512, 16, n))


def unpack_weight(words, scales):
    g, p, n, _ = words.shape
    vals = np.ascontiguousarray(words).view(ml_dtypes.float8_e4m3fn).astype(np.float64) * np.repeat(np.exp2(scales.astype(np.float64) - 127.0), 8, axis=1)[..., None]
    return vals.transpose(0, 1, 3, 2).reshape(g * 512, n)

def planes(y):
    n, m = y.shape
    v = y.astype(np.float32).astype(ml_dtypes.bfloat16).astype(np.float64).reshape(n // 32, 32, m)
    top = np.abs(v).max(1)
    byte = np.clip(np.where(top > 0, np.frexp(top)[1] - 1 + 127 - 7, 1), 1, 254)
    codes = (v * np.exp2(127.0 - byte)[:, None, :]).reshape(n, m).astype(np.float32).astype(ml_dtypes.float8_e4m3fn).view(np.uint8)
    words = codes.reshape(n // 512, 128, 4, m).transpose(0, 1, 3, 2)
    return np.ascontiguousarray(words), np.ascontiguousarray(byte.astype(np.uint8).reshape(n // 512, 16, m))


K, T, S, N, H = 512, 2048, 512, 512, 512


def setup_inputs():
    n = np.random.standard_normal
    s = mx_kscale(K)[:, None]
    u = mx_kscale(S)
    packed_xT = pack_weight(n((K, T)) * s)
    return {
        "x_words": packed_xT[0],
        "x_scales": packed_xT[1],
        "wa": (n((K, H)) / np.sqrt(K) / s).astype(np.float32),
        "wb": (n((K, N)) / np.sqrt(K) / s).astype(np.float32),
        "gt": (np.random.uniform(0.5, 1.5, (S, 1)) * u[:, None]).astype(np.float32),
        "gi": (np.random.uniform(0.5, 1.5, (S, 1)) / u[:, None]).astype(np.float32),
        "offs": striped(np.random.permutation(T)[:S]),
        "two": striped(np.random.permutation(T)[:S]),
        "n1": striped8(np.stack([np.random.permutation(H) for _ in range(8)])),
        "n2": striped8(np.stack([np.random.permutation(H) for _ in range(8)])),
        "n3": striped8(np.stack([np.random.permutation(N) for _ in range(8)])),
        "n4": striped8(np.stack([np.random.permutation(N) for _ in range(8)])),
        "n5": striped8(np.stack([np.random.permutation(N) for _ in range(8)])),
    }


def reference(x_words, x_scales, wa, wb, gt, gi, offs, two, n1, n2, n3, n4, n5):
    xq = unpack_weight(x_words, x_scales)[:, unstriped(offs)]
    a = xq.T @ mxq(f64(wa), 0, "e4m3")
    st = np.maximum(a, a[np.arange(S)[:, None], runs(n1, S)])
    z = f64(gt) * (np.minimum(st, st[np.arange(S)[:, None], runs(n2, S)]))
    x_two = unpack_weight(x_words, x_scales)[:, unstriped(two)]
    b = x_two.T @ mxq(f64(wb), 0, "e4m3")
    z2 = f64(gi) * b
    cv = 0.0625 * ((mxq(z, 0, "e4m3").T @ mxq(z2, 0, "e4m3")))
    out_0 = 0.75 * (cv * (cv[np.arange(H)[:, None], runs(n3, H)]) + (cv[np.arange(H)[:, None], runs(n4, H)]) * (cv[np.arange(H)[:, None], runs(n5, H)]))
    return (out_0,) + planes(out_0)

@@ -1,0 +1,298 @@
+from contextlib import ExitStack
+
+import concourse.mybir as mybir
+from concourse.masks import make_identity
+
+K, T, S, N, H = 512, 2048, 512, 512, 512
+FLOPS = 3 * 2 * 512 * 512 * 512
+
+F32 = mybir.dt.float32
+BF16 = mybir.dt.bfloat16
+I32 = mybir.dt.int32
+U32 = mybir.dt.uint32
+U16 = mybir.dt.uint16
+U8 = mybir.dt.uint8
+FP8X4 = mybir.dt.float8_e4m3fn_x4
+ALU = mybir.AluOpType
+ACT = mybir.ActivationFunctionType
+
+P = 128
+PACK = 4
+PIECES = ((0, 384), (384, 512))
+
+
+def entries(offsets, lo, hi):
+    return offsets[:, lo // 16 : hi // 16]
+
+
+def interleave(engine_copy, dst, src):
+    engine_copy(
+        out=dst.rearrange("p (c i) t -> p c t i", i=4),
+        in_=src.rearrange("p t (c i) -> p c t i", i=4),
+    )
+
+
+def tile_picked_momhopmndot_none_po_kernel(
+    tc, x_words, x_scales, wa, wb, gt, gi, offs, two, n1, n2, n3, n4, n5, out_0, out_1, out_2
+):
+    nc = tc.nc
+    with ExitStack() as ctx:
+        keep = ctx.enter_context(tc.tile_pool(name="keep", bufs=1))
+        psum = ctx.enter_context(tc.psum_pool(name="psum", bufs=1))
+
+        def sb(name, shape, dtype):
+            return keep.tile(shape, dtype, name=name, align_bytes=64)
+
+        def bank(number, name):
+            return psum.tile([P, 512], F32, name=name, tag="bank%d" % number)
+
+        def load_list(name, source):
+            tile = sb(name, [P, S // 16], U16)
+            nc.sync.dma_start(tile[:], source)
+            return tile
+
+        def quantize(codes, scales, grouped, lo, hi):
+            nc.vector.quantize_mx(
+                out=codes[:, lo:hi].bitcast(FP8X4),
+                scales=scales[:, lo:hi],
+                in_=grouped,
+            )
+
+        def product(out, lhs_codes, lhs_scales, t, rhs_codes, rhs_scales):
+            cols = slice(t * P, (t + 1) * P)
+            nc.tensor.matmul_mx(
+                out=out[:],
+                lhsT=lhs_codes[:, cols].bitcast(FP8X4),
+                lhsT_scale=lhs_scales[:, cols],
+                rhs=rhs_codes[:].bitcast(FP8X4),
+                rhs_scale=rhs_scales[:],
+                start=True,
+                stop=True,
+            )
+
+        scale_rows = sb("scale_rows", [P, T // 4], I32)
+        for q in range(4):
+            queue = nc.sync if q < 2 else nc.scalar
+            queue.dma_start(scale_rows[32 * q : 32 * q + 4, :], x_scales[0][4 * q : 4 * q + 4, :].bitcast(I32))
+        table_words = sb("table_words", [P, T], I32)
+        nc.sync.dma_start(table_words[:], x_words[0].rearrange("p c r -> p (c r)").bitcast(I32))
+        offs_l = load_list("offs_l", offs)
+        gain_rows = sb("gain_rows", [8, P], F32)
+        for row, g in ((0, gt), (4, gi)):
+            nc.scalar.dma_start(
+                gain_rows[row : row + 4, :].rearrange("t (q r) -> t q r", r=8),
+                g.rearrange("(q t r) o -> t q (r o)", t=4, r=8),
+            )
+
+        table_scales = sb("table_scales", [P, T], U8)
+        nc.vector.memset(table_scales[:].bitcast(I32), 0)
+        for q in range(4):
+            nc.vector.tensor_copy(table_scales[32 * q : 32 * q + 4, :].bitcast(I32), scale_rows[32 * q : 32 * q + 4, :])
+        gains = sb("gains", [P, P], F32)
+        nc.gpsimd.memset(gains[:], 0.0)
+        warm = sb("warm", [P, 1], F32)
+        nc.scalar.copy(warm[:], gains[:, 0:1])
+        ident = sb("ident", [P, P], F32)
+        make_identity(nc, ident[:])
+        nc.scalar.copy(gains[0:8, :], gain_rows[:])
+
+        def load_weight_half(name, w, half):
+            raw = sb(name, [P, PACK, 256], F32)
+            nc.sync.dma_start(raw[:], w.rearrange("(p j) c -> p j c", j=PACK)[:, :, 256 * half : 256 * (half + 1)])
+            return raw
+
+        wa_raw = [load_weight_half("wa_raw%d" % h, wa, h) for h in range(2)]
+        two_l = load_list("two_l", two)
+        n1_l = load_list("n1_l", n1)
+        wb_raw = [load_weight_half("wb_raw%d" % h, wb, h) for h in range(2)]
+        n2_l = load_list("n2_l", n2)
+        n4_l = load_list("n4_l", n4)
+        n5_l = load_list("n5_l", n5)
+        n3_l = load_list("n3_l", n3)
+
+        gains_ps = bank(7, "gains_ps")
+        nc.tensor.transpose(gains_ps[:, 0:P], gains[:], ident[:])
+        gain_cols = sb("gain_cols", [P, 2 * PACK], F32)
+        nc.scalar.copy(gain_cols[:], gains_ps[:, 0 : 2 * PACK])
+        gt_nonneg = sb("gt_nonneg", [P, PACK], F32)
+        gt_sign = sb("gt_sign", [P, PACK], F32)
+        gt_abs = sb("gt_abs", [P, PACK], F32)
+        gi_signed = sb("gi_signed", [P, PACK], F32)
+        nc.gpsimd.tensor_scalar(gt_nonneg[:], gain_cols[:, 0:PACK], 0.0, 2.0, ALU.is_ge, ALU.mult)
+        nc.gpsimd.tensor_scalar(gt_sign[:], gt_nonneg[:], 1.0, -1.0, ALU.mult, ALU.add)
+        nc.gpsimd.tensor_tensor(gt_abs[:], gain_cols[:, 0:PACK], gt_sign[:], ALU.mult)
+        nc.gpsimd.tensor_tensor(gi_signed[:], gain_cols[:, PACK : 2 * PACK], gt_sign[:], ALU.mult)
+
+        def pick(name, offsets):
+            words = sb(name + "_words", [P, S], U32)
+            nc.vector.tensor_copy(
+                words[:].rearrange("p (t q r) -> p q t r", t=4, r=8),
+                table_words[:].bitcast(U32).indirect(offsets[:]),
+            )
+            listed = sb(name + "_listed", [P, S], U8)
+            nc.vector.tensor_copy(listed[:], table_scales[:].indirect(offsets[:]))
+            scales = sb(name + "_scales", [P, S], U8)
+            nc.vector.tensor_copy(
+                scales[:].bitcast(I32).rearrange("p (t q w) -> p t q w", t=4, w=2),
+                listed[:].bitcast(I32).rearrange("p (q t w) -> p t q w", t=4, w=2),
+            )
+            return words, scales
+
+        def round_weight(name, raw):
+            halves = []
+            for h in range(2):
+                grouped = sb("%s_grouped%d" % (name, h), [P, 256, PACK], BF16)
+                interleave(nc.scalar.copy, grouped[:], raw[h][:])
+                halves.append(grouped)
+            return halves
+
+        def quantize_weight(name, halves):
+            codes = sb(name + "_codes", [P, 512], U32)
+            scales = sb(name + "_scales", [P, 512], U8)
+            for h in range(2):
+                quantize(codes, scales, halves[h][:].rearrange("p c t -> p (c t)"), 256 * h, 256 * (h + 1))
+            return codes, scales
+
+        wa_grouped = round_weight("wa", wa_raw)
+        xa_words, xa_scales = pick("xa", offs_l)
+        wa_codes, wa_scales = quantize_weight("wa", wa_grouped)
+        xb_words, xb_scales = pick("xb", two_l)
+
+        a_rows = []
+        for t in range(PACK):
+            acc = bank(t, "a_ps%d" % t)
+            product(acc, xa_words, xa_scales, t, wa_codes, wa_scales)
+            rows = sb("a_rows%d" % t, [P, H], F32)
+            nc.scalar.activation(rows[:], acc[:], ACT.Copy, scale=gt_abs[:, t : t + 1])
+            a_rows.append(rows)
+
+        wb_grouped = round_weight("wb", wb_raw)
+
+        st_rows = [sb("st_rows%d" % t, [P, H], F32) for t in range(PACK)]
+        a_n1 = [sb("a_n1_%d" % t, [P, H], F32) for t in range(PACK)]
+
+        def fetch_n1(t):
+            for lo, hi in ((0, 256), (256, 512)):
+                nc.vector.tensor_copy(a_n1[t][:, lo:hi], a_rows[t][:].indirect(entries(n1_l, lo, hi)))
+
+        def larger(t):
+            nc.vector.tensor_tensor(st_rows[t][:], a_rows[t][:], a_n1[t][:], ALU.max)
+
+        fetch_n1(0)
+        fetch_n1(1)
+        larger(0)
+        fetch_n1(2)
+        larger(1)
+        wb_codes, wb_scales = quantize_weight("wb", wb_grouped)
+        fetch_n1(3)
+        larger(2)
+
+        z2_rows = sb("z2_rows", [P, PACK, N], BF16)
+        for t in range(PACK):
+            acc = bank(4 + t, "b_ps%d" % t)
+            product(acc, xb_words, xb_scales, t, wb_codes, wb_scales)
+            nc.scalar.activation(z2_rows[:, t, :], acc[:], ACT.Copy, scale=gi_signed[:, t : t + 1])
+        z2_grouped = sb("z2_grouped", [P, N, PACK], BF16)
+        interleave(nc.scalar.copy, z2_grouped[:], z2_rows[:])
+
+        z_grouped = sb("z_grouped", [P, PACK, P, PACK], BF16)
+        z_rows = [sb("z_rows%d" % i, [P, PACK, hi - lo], BF16) for i, (lo, hi) in enumerate(PIECES)]
+        st_n2 = [sb("st_n2_%d" % i, [P, PACK, hi - lo], F32) for i, (lo, hi) in enumerate(PIECES)]
+
+        def fetch_n2(i, t):
+            lo, hi = PIECES[i]
+            nc.vector.tensor_copy(st_n2[i][:, t, :], st_rows[t][:].indirect(entries(n2_l, lo, hi)))
+
+        def smaller(i, t):
+            lo, hi = PIECES[i]
+            nc.vector.tensor_tensor(z_rows[i][:, t, :], st_rows[t][:, lo:hi], st_n2[i][:, t, :], ALU.min)
+
+        def deal_z(engine_copy, i):
+            lo, hi = PIECES[i]
+            engine_copy(
+                out=z_grouped[:, :, lo // 4 : hi // 4, :].rearrange("p u m t -> p m t u"),
+                in_=z_rows[i][:].rearrange("p t (m u) -> p m t u", u=4),
+            )
+
+        fetch_n2(0, 0)
+        larger(3)
+        for t in range(1, PACK):
+            fetch_n2(0, t)
+            smaller(0, t - 1)
+        fetch_n2(1, 0)
+        smaller(0, 3)
+        deal_z(nc.scalar.copy, 0)
+        for t in range(1, PACK):
+            fetch_n2(1, t)
+            smaller(1, t - 1)
+        z2_codes = sb("z2_codes", [P, N], U32)
+        z2_scales = sb("z2_scales", [P, N], U8)
+        quantize(z2_codes, z2_scales, z2_grouped[:].rearrange("p c t -> p (c t)"), 0, N)
+        smaller(1, 3)
+        deal_z(nc.vector.tensor_copy, 1)
+
+        z_codes = sb("z_codes", [P, H], U32)
+        z_scales = sb("z_scales", [P, H], U8)
+        cv_rows, cv_part = [], []
+        for u in range(PACK):
+            quantize(z_codes, z_scales, z_grouped[:, u, :, :].rearrange("p m t -> p (m t)"), u * P, (u + 1) * P)
+            acc = bank(u, "cv_ps%d" % u)
+            product(acc, z_codes, z_scales, u, z2_codes, z2_scales)
+            part = sb("cv_part%d" % u, [P, N], F32)
+            nc.scalar.activation(part[:], acc[:], ACT.Copy, scale=0.75 * 0.0625)
+            rows = sb("cv_rows%d" % u, [P, N], F32)
+            nc.scalar.activation(rows[:], acc[:], ACT.Copy, scale=0.0625)
+            cv_rows.append(rows)
+            cv_part.append(part)
+
+        out_codes = sb("out_codes", [P, N], U32)
+        out_scales = sb("out_scales", [P, N], U8)
+        out_view = out_0.rearrange("(p u) n -> p u n", u=PACK)
+        words_view = out_1[0].rearrange("p c r -> p (c r)").bitcast(I32)
+        cv_n4 = [sb("cv_n4_%d" % i, [P, PACK, hi - lo], F32) for i, (lo, hi) in enumerate(PIECES)]
+        prod45 = [sb("prod45_%d" % i, [P, PACK, hi - lo], F32) for i, (lo, hi) in enumerate(PIECES)]
+        prod3 = [sb("prod3_%d" % i, [P, PACK, hi - lo], F32) for i, (lo, hi) in enumerate(PIECES)]
+        result = [sb("result%d" % i, [P, PACK, hi - lo], F32) for i, (lo, hi) in enumerate(PIECES)]
+        out_grouped = [sb("out_grouped%d" % i, [P, hi - lo, PACK], BF16) for i, (lo, hi) in enumerate(PIECES)]
+
+        def products(i, u):
+            lo, hi = PIECES[i]
+            nc.vector.tensor_copy(cv_n4[i][:, u, :], cv_part[u][:].indirect(entries(n4_l, lo, hi)))
+            nc.vector.tensor_tensor(
+                prod3[i][:, u, :], cv_rows[u][:].indirect(entries(n3_l, lo, hi)), cv_part[u][:, lo:hi], ALU.mult
+            )
+            nc.vector.tensor_tensor(
+                prod45[i][:, u, :], cv_rows[u][:].indirect(entries(n5_l, lo, hi)), cv_n4[i][:, u, :], ALU.mult
+            )
+
+        def add(i, us):
+            nc.vector.tensor_tensor(result[i][:, us, :], prod3[i][:, us, :], prod45[i][:, us, :], ALU.add)
+
+        def quantize_out(i, lo, hi):
+            first = PIECES[i][0]
+            quantize(out_codes, out_scales, out_grouped[i][:, lo - first : hi - first, :].rearrange("p c t -> p (c t)"), lo, hi)
+
+        for u in range(PACK):
+            products(0, u)
+        products(1, 0)
+        add(0, slice(0, 4))
+        nc.sync.dma_start(out_view[:, :, 0:384], result[0][:])
+        interleave(nc.scalar.copy, out_grouped[0][:], result[0][:])
+        products(1, 1)
+        products(1, 2)
+        products(1, 3)
+        add(1, slice(0, 3))
+        add(1, slice(3, 4))
+        nc.sync.dma_start(out_view[:, :, 384:512], result[1][:])
+        quantize_out(0, 0, 256)
+        interleave(nc.vector.tensor_copy, out_grouped[1][:], result[1][:])
+        quantize_out(0, 256, 384)
+        nc.sync.dma_start(words_view[:, 0:384], out_codes[:, 0:384].bitcast(I32))
+        quantize_out(1, 384, 512)
+        nc.sync.dma_start(words_view[:, 384:512], out_codes[:, 384:512].bitcast(I32))
+        for q in range(4):
+            queue = nc.scalar if q % 2 == 0 else nc.sync
+            queue.dma_start(
+                out_2[0][4 * q : 4 * q + 4, :].bitcast(I32),
+                out_scales[32 * q : 32 * q + 4, :].bitcast(I32),
+            )

@@ -40,8 +40,8 @@ def tile_picked_momhopmndot_none_po_kernel(
         keep = ctx.enter_context(tc.tile_pool(name="keep", bufs=1))
         psum = ctx.enter_context(tc.psum_pool(name="psum", bufs=1))
 
-        def sb(name, shape, dtype):
-            return keep.tile(shape, dtype, name=name, align_bytes=64)
+        def sb(name, shape, dtype, tag=None):
+            return keep.tile(shape, dtype, name=name, tag=tag or name, align_bytes=64)
 
         def bank(number, name):
             return psum.tile([P, 512], F32, name=name, tag="bank%d" % number)
@@ -58,85 +58,86 @@ def tile_picked_momhopmndot_none_po_kernel(
                 in_=grouped,
             )
 
-        def product(out, lhs_codes, lhs_scales, t, rhs_codes, rhs_scales):
+        def product(out, lhs_codes, lhs_scales, t, rhs_codes, rhs_scales, lo=0, hi=512):
             cols = slice(t * P, (t + 1) * P)
             nc.tensor.matmul_mx(
-                out=out[:],
+                out=out[:, 0 : hi - lo],
                 lhsT=lhs_codes[:, cols].bitcast(FP8X4),
                 lhsT_scale=lhs_scales[:, cols],
-                rhs=rhs_codes[:].bitcast(FP8X4),
-                rhs_scale=rhs_scales[:],
+                rhs=rhs_codes[:, lo:hi].bitcast(FP8X4),
+                rhs_scale=rhs_scales[:, lo:hi],
                 start=True,
                 stop=True,
             )
-
-        scale_rows = sb("scale_rows", [P, T // 4], I32)
-        for q in range(4):
-            queue = nc.sync if q < 2 else nc.scalar
-            queue.dma_start(scale_rows[32 * q : 32 * q + 4, :], x_scales[0][4 * q : 4 * q + 4, :].bitcast(I32))
-        table_words = sb("table_words", [P, T], I32)
-        nc.sync.dma_start(table_words[:], x_words[0].rearrange("p c r -> p (c r)").bitcast(I32))
-        offs_l = load_list("offs_l", offs)
-        gain_rows = sb("gain_rows", [8, P], F32)
-        for row, g in ((0, gt), (4, gi)):
-            nc.scalar.dma_start(
-                gain_rows[row : row + 4, :].rearrange("t (q r) -> t q r", r=8),
-                g.rearrange("(q t r) o -> t q (r o)", t=4, r=8),
-            )
-
-        table_scales = sb("table_scales", [P, T], U8)
-        nc.vector.memset(table_scales[:].bitcast(I32), 0)
-        for q in range(4):
-            nc.vector.tensor_copy(table_scales[32 * q : 32 * q + 4, :].bitcast(I32), scale_rows[32 * q : 32 * q + 4, :])
-        gains = sb("gains", [P, P], F32)
-        nc.gpsimd.memset(gains[:], 0.0)
-        warm = sb("warm", [P, 1], F32)
-        nc.scalar.copy(warm[:], gains[:, 0:1])
-        ident = sb("ident", [P, P], F32)
-        make_identity(nc, ident[:])
-        nc.scalar.copy(gains[0:8, :], gain_rows[:])
 
         def load_weight_half(name, w, half):
             raw = sb(name, [P, PACK, 256], F32)
             nc.sync.dma_start(raw[:], w.rearrange("(p j) c -> p j c", j=PACK)[:, :, 256 * half : 256 * (half + 1)])
             return raw
 
-        wa_raw = [load_weight_half("wa_raw%d" % h, wa, h) for h in range(2)]
+        scale_rows = sb("scale_rows", [P, T // 4], I32)
+        for q in range(4):
+            queue = nc.sync if q < 2 else nc.scalar
+            queue.dma_start(scale_rows[32 * q : 32 * q + 4, :], x_scales[0][4 * q : 4 * q + 4, :].bitcast(I32))
+        offs_l = load_list("offs_l", offs)
+        gains = sb("gains", [P, P], F32)
+        nc.gpsimd.memset(gains[:], 0.0)
         two_l = load_list("two_l", two)
+        wa_raw = [load_weight_half("wa_raw%d" % h, wa, h) for h in range(2)]
+        for row, g in ((0, gt), (4, gi)):
+            nc.sync.dma_start(
+                gains[row : row + 4, :].rearrange("t (q r) -> t q r", r=8),
+                g.rearrange("(q t r) o -> t q (r o)", t=4, r=8),
+            )
+        table_words = sb("table_words", [P, T], I32)
+        nc.sync.dma_start(table_words[:], x_words[0].rearrange("p c r -> p (c r)").bitcast(I32))
         n1_l = load_list("n1_l", n1)
         wb_raw = [load_weight_half("wb_raw%d" % h, wb, h) for h in range(2)]
         n2_l = load_list("n2_l", n2)
         n4_l = load_list("n4_l", n4)
-        n5_l = load_list("n5_l", n5)
         n3_l = load_list("n3_l", n3)
+        n5_l = load_list("n5_l", n5)
+
+        table_scales = sb("table_scales", [P, T], U8)
+        nc.vector.memset(table_scales[:].bitcast(I32), 0)
+        for q in range(4):
+            nc.vector.tensor_copy(table_scales[32 * q : 32 * q + 4, :].bitcast(I32), scale_rows[32 * q : 32 * q + 4, :])
+        ident = sb("ident", [P, P], F32)
+        make_identity(nc, ident[:])
+        warm = sb("warm", [P, 1], F32)
+        nc.scalar.copy(warm[:], ident[:, 0:1])
 
         gains_ps = bank(7, "gains_ps")
         nc.tensor.transpose(gains_ps[:, 0:P], gains[:], ident[:])
-        gain_cols = sb("gain_cols", [P, 2 * PACK], F32)
-        nc.scalar.copy(gain_cols[:], gains_ps[:, 0 : 2 * PACK])
-        gt_nonneg = sb("gt_nonneg", [P, PACK], F32)
-        gt_sign = sb("gt_sign", [P, PACK], F32)
         gt_abs = sb("gt_abs", [P, PACK], F32)
+        gt_sign = sb("gt_sign", [P, PACK], F32)
+        gi_cols = sb("gi_cols", [P, PACK], F32)
         gi_signed = sb("gi_signed", [P, PACK], F32)
-        nc.gpsimd.tensor_scalar(gt_nonneg[:], gain_cols[:, 0:PACK], 0.0, 2.0, ALU.is_ge, ALU.mult)
-        nc.gpsimd.tensor_scalar(gt_sign[:], gt_nonneg[:], 1.0, -1.0, ALU.mult, ALU.add)
-        nc.gpsimd.tensor_tensor(gt_abs[:], gain_cols[:, 0:PACK], gt_sign[:], ALU.mult)
-        nc.gpsimd.tensor_tensor(gi_signed[:], gain_cols[:, PACK : 2 * PACK], gt_sign[:], ALU.mult)
+        nc.scalar.activation(gt_abs[:], gains_ps[:, 0:PACK], ACT.Abs)
+        nc.scalar.activation(gt_sign[:], gains_ps[:, 0:PACK], ACT.Sign)
+        nc.scalar.copy(gi_cols[:], gains_ps[:, PACK : 2 * PACK])
+        nc.gpsimd.tensor_tensor(gi_signed[:], gi_cols[:], gt_sign[:], ALU.mult)
 
-        def pick(name, offsets):
-            words = sb(name + "_words", [P, S], U32)
+        def pick_words(name, offsets):
+            words = sb(name, [P, S], U32)
             nc.vector.tensor_copy(
                 words[:].rearrange("p (t q r) -> p q t r", t=4, r=8),
                 table_words[:].bitcast(U32).indirect(offsets[:]),
             )
+            return words
+
+        def pick_scales(name, offsets):
             listed = sb(name + "_listed", [P, S], U8)
             nc.vector.tensor_copy(listed[:], table_scales[:].indirect(offsets[:]))
-            scales = sb(name + "_scales", [P, S], U8)
+            return listed
+
+        def deal_scales(name, listed):
+            scales = sb(name, [P, S], U8)
             nc.vector.tensor_copy(
                 scales[:].bitcast(I32).rearrange("p (t q w) -> p t q w", t=4, w=2),
                 listed[:].bitcast(I32).rearrange("p (q t w) -> p t q w", t=4, w=2),
             )
-            return words, scales
+            return scales
 
         def round_weight(name, raw):
             halves = []
@@ -154,29 +155,38 @@ def tile_picked_momhopmndot_none_po_kernel(
             return codes, scales
 
         wa_grouped = round_weight("wa", wa_raw)
-        xa_words, xa_scales = pick("xa", offs_l)
+        xa_listed = pick_scales("xa", offs_l)
+        xb_listed = pick_scales("xb", two_l)
+        xa_scales = deal_scales("xa_scales", xa_listed)
         wa_codes, wa_scales = quantize_weight("wa", wa_grouped)
-        xb_words, xb_scales = pick("xb", two_l)
+        xb_scales = deal_scales("xb_scales", xb_listed)
+        xa_words = pick_words("xa_words", offs_l)
+        xb_words = pick_words("xb_words", two_l)
 
-        a_rows = []
-        for t in range(PACK):
+        halves = ((0, 256), (256, 512))
+        a_rows = [sb("a_rows%d" % t, [P, H], F32) for t in range(PACK)]
+        for number, (lo, hi) in zip((0, 4), halves):
+            acc = bank(number, "a_ps0_%d" % lo)
+            product(acc, xa_words, xa_scales, 0, wa_codes, wa_scales, lo, hi)
+            nc.scalar.activation(a_rows[0][:, lo:hi], acc[:, 0:256], ACT.Copy, scale=gt_abs[:, 0:1])
+        for t in range(1, PACK):
             acc = bank(t, "a_ps%d" % t)
             product(acc, xa_words, xa_scales, t, wa_codes, wa_scales)
-            rows = sb("a_rows%d" % t, [P, H], F32)
-            nc.scalar.activation(rows[:], acc[:], ACT.Copy, scale=gt_abs[:, t : t + 1])
-            a_rows.append(rows)
+            nc.scalar.activation(a_rows[t][:], acc[:], ACT.Copy, scale=gt_abs[:, t : t + 1])
 
         wb_grouped = round_weight("wb", wb_raw)
 
         st_rows = [sb("st_rows%d" % t, [P, H], F32) for t in range(PACK)]
         a_n1 = [sb("a_n1_%d" % t, [P, H], F32) for t in range(PACK)]
+        st_rounded = sb("st_rounded", [P, PACK, H], BF16)
 
         def fetch_n1(t):
-            for lo, hi in ((0, 256), (256, 512)):
+            for lo, hi in halves:
                 nc.vector.tensor_copy(a_n1[t][:, lo:hi], a_rows[t][:].indirect(entries(n1_l, lo, hi)))
 
         def larger(t):
             nc.vector.tensor_tensor(st_rows[t][:], a_rows[t][:], a_n1[t][:], ALU.max)
+            nc.scalar.copy(st_rounded[:, t, :], st_rows[t][:])
 
         fetch_n1(0)
         fetch_n1(1)
@@ -184,110 +194,135 @@ def tile_picked_momhopmndot_none_po_kernel(
         fetch_n1(2)
         larger(1)
         wb_codes, wb_scales = quantize_weight("wb", wb_grouped)
-        fetch_n1(3)
-        larger(2)
-
         z2_rows = sb("z2_rows", [P, PACK, N], BF16)
         for t in range(PACK):
             acc = bank(4 + t, "b_ps%d" % t)
             product(acc, xb_words, xb_scales, t, wb_codes, wb_scales)
             nc.scalar.activation(z2_rows[:, t, :], acc[:], ACT.Copy, scale=gi_signed[:, t : t + 1])
-        z2_grouped = sb("z2_grouped", [P, N, PACK], BF16)
-        interleave(nc.scalar.copy, z2_grouped[:], z2_rows[:])
+        fetch_n1(3)
+        larger(2)
 
         z_grouped = sb("z_grouped", [P, PACK, P, PACK], BF16)
-        z_rows = [sb("z_rows%d" % i, [P, PACK, hi - lo], BF16) for i, (lo, hi) in enumerate(PIECES)]
-        st_n2 = [sb("st_n2_%d" % i, [P, PACK, hi - lo], F32) for i, (lo, hi) in enumerate(PIECES)]
+        z_rows = [sb("z_rows%d" % i, [P, PACK, 256], BF16) for i in range(2)]
+        st_n2 = [sb("st_n2_0", [P, PACK, 256], BF16)]
 
         def fetch_n2(i, t):
-            lo, hi = PIECES[i]
+            lo, hi = halves[i]
             nc.vector.tensor_copy(st_n2[i][:, t, :], st_rows[t][:].indirect(entries(n2_l, lo, hi)))
 
-        def smaller(i, t):
-            lo, hi = PIECES[i]
-            nc.vector.tensor_tensor(z_rows[i][:, t, :], st_rows[t][:, lo:hi], st_n2[i][:, t, :], ALU.min)
+        def smaller(i, ts):
+            lo, hi = halves[i]
+            nc.vector.tensor_tensor(z_rows[i][:, ts, :], st_rounded[:, ts, lo:hi], st_n2[i][:, ts, :], ALU.min)
 
-        def deal_z(engine_copy, i):
-            lo, hi = PIECES[i]
+        def deal_z(engine_copy, i, us):
+            lo, hi = halves[i]
             engine_copy(
-                out=z_grouped[:, :, lo // 4 : hi // 4, :].rearrange("p u m t -> p m t u"),
-                in_=z_rows[i][:].rearrange("p t (m u) -> p m t u", u=4),
+                out=z_grouped[:, us, lo // 4 : hi // 4, :].rearrange("p u m t -> p m t u"),
+                in_=z_rows[i][:].rearrange("p t (m u) -> p m t u", u=4)[:, :, :, us],
             )
 
         fetch_n2(0, 0)
         larger(3)
+        z2_grouped = sb("z2_grouped", [P, N, PACK], BF16)
+        interleave(nc.scalar.copy, z2_grouped[:], z2_rows[:])
+        st_n2.append(sb("st_n2_1", [P, PACK, 256], BF16, tag="a_n1_3"))
         for t in range(1, PACK):
             fetch_n2(0, t)
-            smaller(0, t - 1)
         fetch_n2(1, 0)
-        smaller(0, 3)
-        deal_z(nc.scalar.copy, 0)
+        smaller(0, slice(0, 4))
+        deal_z(nc.scalar.copy, 0, slice(0, 4))
         for t in range(1, PACK):
             fetch_n2(1, t)
-            smaller(1, t - 1)
         z2_codes = sb("z2_codes", [P, N], U32)
         z2_scales = sb("z2_scales", [P, N], U8)
+        smaller(1, slice(0, 3))
+        smaller(1, slice(3, 4))
         quantize(z2_codes, z2_scales, z2_grouped[:].rearrange("p c t -> p (c t)"), 0, N)
-        smaller(1, 3)
-        deal_z(nc.vector.tensor_copy, 1)
+        deal_z(nc.vector.tensor_copy, 1, slice(0, 1))
+        deal_z(nc.scalar.copy, 1, slice(1, 4))
 
         z_codes = sb("z_codes", [P, H], U32)
         z_scales = sb("z_scales", [P, H], U8)
-        cv_rows, cv_part = [], []
-        for u in range(PACK):
+        cv_rows = [sb("cv_rows%d" % u, [P, N], F32) for u in range(PACK)]
+        cv_part = [sb("cv_part%d" % u, [P, N], F32) for u in range(PACK)]
+
+        def quantize_z(u):
             quantize(z_codes, z_scales, z_grouped[:, u, :, :].rearrange("p m t -> p (m t)"), u * P, (u + 1) * P)
+
+        quantize_z(0)
+        first = [bank(0, "cv_ps0_lo"), bank(4, "cv_ps0_hi")]
+        for acc, (lo, hi) in zip(first, halves):
+            product(acc, z_codes, z_scales, 0, z2_codes, z2_scales, lo, hi)
+        nc.scalar.activation(cv_part[0][:, 0:256], first[0][:, 0:256], ACT.Copy, scale=0.75 * 0.0625)
+        for u in range(1, PACK):
+            quantize_z(u)
+        nc.vector.tensor_scalar(cv_part[0][:, 256:512], first[1][:, 0:256], 0.75 * 0.0625, None, ALU.mult)
+        for acc, (lo, hi) in zip(first, halves):
+            nc.scalar.activation(cv_rows[0][:, lo:hi], acc[:, 0:256], ACT.Copy, scale=0.0625)
+        for u in range(1, PACK):
             acc = bank(u, "cv_ps%d" % u)
             product(acc, z_codes, z_scales, u, z2_codes, z2_scales)
-            part = sb("cv_part%d" % u, [P, N], F32)
-            nc.scalar.activation(part[:], acc[:], ACT.Copy, scale=0.75 * 0.0625)
-            rows = sb("cv_rows%d" % u, [P, N], F32)
-            nc.scalar.activation(rows[:], acc[:], ACT.Copy, scale=0.0625)
-            cv_rows.append(rows)
-            cv_part.append(part)
+            nc.scalar.activation(cv_part[u][:], acc[:], ACT.Copy, scale=0.75 * 0.0625)
+            nc.scalar.activation(cv_rows[u][:], acc[:], ACT.Copy, scale=0.0625)
 
         out_codes = sb("out_codes", [P, N], U32)
         out_scales = sb("out_scales", [P, N], U8)
         out_view = out_0.rearrange("(p u) n -> p u n", u=PACK)
         words_view = out_1[0].rearrange("p c r -> p (c r)").bitcast(I32)
-        cv_n4 = [sb("cv_n4_%d" % i, [P, PACK, hi - lo], F32) for i, (lo, hi) in enumerate(PIECES)]
-        prod45 = [sb("prod45_%d" % i, [P, PACK, hi - lo], F32) for i, (lo, hi) in enumerate(PIECES)]
-        prod3 = [sb("prod3_%d" % i, [P, PACK, hi - lo], F32) for i, (lo, hi) in enumerate(PIECES)]
         result = [sb("result%d" % i, [P, PACK, hi - lo], F32) for i, (lo, hi) in enumerate(PIECES)]
         out_grouped = [sb("out_grouped%d" % i, [P, hi - lo, PACK], BF16) for i, (lo, hi) in enumerate(PIECES)]
 
-        def products(i, u):
-            lo, hi = PIECES[i]
-            nc.vector.tensor_copy(cv_n4[i][:, u, :], cv_part[u][:].indirect(entries(n4_l, lo, hi)))
-            nc.vector.tensor_tensor(
-                prod3[i][:, u, :], cv_rows[u][:].indirect(entries(n3_l, lo, hi)), cv_part[u][:, lo:hi], ALU.mult
-            )
-            nc.vector.tensor_tensor(
-                prod45[i][:, u, :], cv_rows[u][:].indirect(entries(n5_l, lo, hi)), cv_n4[i][:, u, :], ALU.mult
-            )
+        def fetch_n4(dst, u, lo, hi):
+            nc.vector.tensor_copy(dst, cv_part[u][:].indirect(entries(n4_l, lo, hi)))
 
-        def add(i, us):
-            nc.vector.tensor_tensor(result[i][:, us, :], prod3[i][:, us, :], prod45[i][:, us, :], ALU.add)
+        def times_n3(dst, u, lo, hi):
+            nc.vector.tensor_tensor(dst, cv_rows[u][:].indirect(entries(n3_l, lo, hi)), cv_part[u][:, lo:hi], ALU.mult)
+
+        def times_n5(dst, u, lo, hi, fetched):
+            nc.vector.tensor_tensor(dst, cv_rows[u][:].indirect(entries(n5_l, lo, hi)), fetched, ALU.mult)
 
         def quantize_out(i, lo, hi):
-            first = PIECES[i][0]
-            quantize(out_codes, out_scales, out_grouped[i][:, lo - first : hi - first, :].rearrange("p c t -> p (c t)"), lo, hi)
+            start = PIECES[i][0]
+            quantize(out_codes, out_scales, out_grouped[i][:, lo - start : hi - start, :].rearrange("p c t -> p (c t)"), lo, hi)
 
+        lo, hi = PIECES[0]
         for u in range(PACK):
-            products(0, u)
-        products(1, 0)
-        add(0, slice(0, 4))
-        nc.sync.dma_start(out_view[:, :, 0:384], result[0][:])
-        interleave(nc.scalar.copy, out_grouped[0][:], result[0][:])
-        products(1, 1)
-        products(1, 2)
-        products(1, 3)
-        add(1, slice(0, 3))
-        add(1, slice(3, 4))
-        nc.sync.dma_start(out_view[:, :, 384:512], result[1][:])
+            cv_n4 = sb("cv_n4_%d" % u, [P, hi - lo], F32)
+            prod3 = sb("prod3_%d" % u, [P, hi - lo], F32)
+            prod45 = sb("prod45_%d" % u, [P, hi - lo], F32)
+            fetch_n4(cv_n4[:], u, lo, hi)
+            times_n3(prod3[:], u, lo, hi)
+            times_n5(prod45[:], u, lo, hi, cv_n4[:])
+            turned_ps = bank(4 + u % 2, "turned_ps%d" % u)
+            for b in range(3):
+                cols = slice(b * P, (b + 1) * P)
+                nc.tensor.matmul(turned_ps[:, cols], prod3[:, cols], ident[:], start=True, stop=False, is_transpose=True)
+                nc.tensor.matmul(turned_ps[:, cols], prod45[:, cols], ident[:], start=False, stop=True, is_transpose=True)
+            turned = sb("turned%d" % u, [P, hi - lo], F32)
+            nc.scalar.copy(turned[:], turned_ps[:, 0 : hi - lo])
+            back_ps = bank(6 + u % 2, "back_ps%d" % u)
+            for b in range(3):
+                cols = slice(b * P, (b + 1) * P)
+                nc.tensor.transpose(back_ps[:, cols], turned[:, cols], ident[:])
+            nc.scalar.copy(result[0][:, u, :], back_ps[:, 0 : hi - lo])
+            nc.sync.dma_start(out_view[:, u, lo:hi], result[0][:, u, :])
+        interleave(nc.scalar.copy, out_grouped[0][:, 0:256, :], result[0][:, :, 0:256])
+        interleave(nc.scalar.copy, out_grouped[0][:, 256:384, :], result[0][:, :, 256:384])
+
+        lo, hi = PIECES[1]
+        last = sb("last", [P, 2, PACK, hi - lo], F32, tag="cv_n4_2")
+        last45 = sb("last45", [P, PACK, hi - lo], F32)
+        for u in range(PACK):
+            fetch_n4(last[:, 0, u, :], u, lo, hi)
+            times_n3(last[:, 1, u, :], u, lo, hi)
+        for u in range(PACK):
+            times_n5(last45[:, u, :], u, lo, hi, last[:, 0, u, :])
         quantize_out(0, 0, 256)
-        interleave(nc.vector.tensor_copy, out_grouped[1][:], result[1][:])
+        nc.vector.tensor_tensor(result[1][:], last[:, 1, :, :], last45[:], ALU.add)
+        nc.sync.dma_start(out_view[:, :, lo:hi], result[1][:])
         quantize_out(0, 256, 384)
         nc.sync.dma_start(words_view[:, 0:384], out_codes[:, 0:384].bitcast(I32))
+        interleave(nc.vector.tensor_copy, out_grouped[1][:], result[1][:])
         quantize_out(1, 384, 512)
         nc.sync.dma_start(words_view[:, 384:512], out_codes[:, 384:512].bitcast(I32))
         for q in range(4):

@@ -18,7 +18,8 @@ ACT = mybir.ActivationFunctionType
 
 P = 128
 PACK = 4
-PIECES = ((0, 384), (384, 512))
+HALVES = ((0, 256), (256, 512))
+PIECES = ((0, 256), (256, 384), (384, 512))
 
 
 def entries(offsets, lo, hi):
@@ -70,9 +71,11 @@ def tile_picked_momhopmndot_none_po_kernel(
                 stop=True,
             )
 
-        def load_weight_half(name, w, half):
-            raw = sb(name, [P, PACK, 256], F32)
-            nc.sync.dma_start(raw[:], w.rearrange("(p j) c -> p j c", j=PACK)[:, :, 256 * half : 256 * (half + 1)])
+        a_win = [sb("a_win%d" % t, [P, 2 * H], F32) for t in range(PACK)]
+
+        def load_weight(space, w, lo, hi):
+            raw = space.rearrange("p (j c) -> p j c", j=PACK)
+            nc.sync.dma_start(raw, w.rearrange("(p j) c -> p j c", j=PACK)[:, :, lo:hi])
             return raw
 
         scale_rows = sb("scale_rows", [P, T // 4], I32)
@@ -83,7 +86,7 @@ def tile_picked_momhopmndot_none_po_kernel(
         gains = sb("gains", [P, P], F32)
         nc.gpsimd.memset(gains[:], 0.0)
         two_l = load_list("two_l", two)
-        wa_raw = [load_weight_half("wa_raw%d" % h, wa, h) for h in range(2)]
+        wa_raw = [load_weight(a_win[0][:], wa, 0, 256), load_weight(a_win[1][:], wa, 256, 512)]
         for row, g in ((0, gt), (4, gi)):
             nc.sync.dma_start(
                 gains[row : row + 4, :].rearrange("t (q r) -> t q r", r=8),
@@ -92,7 +95,8 @@ def tile_picked_momhopmndot_none_po_kernel(
         table_words = sb("table_words", [P, T], I32)
         nc.sync.dma_start(table_words[:], x_words[0].rearrange("p c r -> p (c r)").bitcast(I32))
         n1_l = load_list("n1_l", n1)
-        wb_raw = [load_weight_half("wb_raw%d" % h, wb, h) for h in range(2)]
+        wb_space = [a_win[2][:, H : 2 * H], a_win[3][:, H : 2 * H], a_win[2][:, 0:H], a_win[3][:, 0:H]]
+        wb_raw = [load_weight(wb_space[i], wb, P * i, P * (i + 1)) for i in range(4)]
         n2_l = load_list("n2_l", n2)
         n4_l = load_list("n4_l", n4)
         n3_l = load_list("n3_l", n3)
@@ -139,192 +143,193 @@ def tile_picked_momhopmndot_none_po_kernel(
             )
             return scales
 
-        def round_weight(name, raw):
-            halves = []
-            for h in range(2):
-                grouped = sb("%s_grouped%d" % (name, h), [P, 256, PACK], BF16)
-                interleave(nc.scalar.copy, grouped[:], raw[h][:])
-                halves.append(grouped)
-            return halves
+        def quantize_half(codes, scales, grouped, half):
+            lo, hi = HALVES[half]
+            quantize(codes, scales, grouped[:].rearrange("p c t -> p (c t)"), lo, hi)
 
-        def quantize_weight(name, halves):
-            codes = sb(name + "_codes", [P, 512], U32)
-            scales = sb(name + "_scales", [P, 512], U8)
-            for h in range(2):
-                quantize(codes, scales, halves[h][:].rearrange("p c t -> p (c t)"), 256 * h, 256 * (h + 1))
-            return codes, scales
+        wa_grouped = [sb("wa_grouped%d" % h, [P, 256, PACK], BF16) for h in range(2)]
+        wb_grouped = [sb("wb_grouped%d" % h, [P, 256, PACK], BF16) for h in range(2)]
+        wa_codes, wa_scales = sb("wa_codes", [P, H], U32), sb("wa_scales", [P, H], U8)
+        wb_codes, wb_scales = sb("wb_codes", [P, N], U32), sb("wb_scales", [P, N], U8)
 
-        wa_grouped = round_weight("wa", wa_raw)
+        for h in range(2):
+            interleave(nc.scalar.copy, wa_grouped[h][:], wa_raw[h])
         xa_listed = pick_scales("xa", offs_l)
         xb_listed = pick_scales("xb", two_l)
         xa_scales = deal_scales("xa_scales", xa_listed)
-        wa_codes, wa_scales = quantize_weight("wa", wa_grouped)
+        for h in range(2):
+            quantize_half(wa_codes, wa_scales, wa_grouped[h], h)
         xb_scales = deal_scales("xb_scales", xb_listed)
         xa_words = pick_words("xa_words", offs_l)
         xb_words = pick_words("xb_words", two_l)
 
-        halves = ((0, 256), (256, 512))
-        a_rows = [sb("a_rows%d" % t, [P, H], F32) for t in range(PACK)]
-        for number, (lo, hi) in zip((0, 4), halves):
+        for number, (lo, hi) in zip((0, 4), HALVES):
             acc = bank(number, "a_ps0_%d" % lo)
             product(acc, xa_words, xa_scales, 0, wa_codes, wa_scales, lo, hi)
-            nc.scalar.activation(a_rows[0][:, lo:hi], acc[:, 0:256], ACT.Copy, scale=gt_abs[:, 0:1])
+            nc.scalar.activation(a_win[0][:, lo:hi], acc[:, 0:256], ACT.Copy, scale=gt_abs[:, 0:1])
+        for i in range(4):
+            interleave(nc.scalar.copy, wb_grouped[i // 2][:, P * (i % 2) : P * (i % 2 + 1), :], wb_raw[i])
+        for h in range(2):
+            quantize_half(wb_codes, wb_scales, wb_grouped[h], h)
         for t in range(1, PACK):
             acc = bank(t, "a_ps%d" % t)
             product(acc, xa_words, xa_scales, t, wa_codes, wa_scales)
-            nc.scalar.activation(a_rows[t][:], acc[:], ACT.Copy, scale=gt_abs[:, t : t + 1])
+            nc.scalar.activation(a_win[t][:, 0:H], acc[:], ACT.Copy, scale=gt_abs[:, t : t + 1])
 
-        wb_grouped = round_weight("wb", wb_raw)
-
-        st_rows = [sb("st_rows%d" % t, [P, H], F32) for t in range(PACK)]
-        a_n1 = [sb("a_n1_%d" % t, [P, H], F32) for t in range(PACK)]
+        st_win = [sb("st_win%d" % t, [P, 2 * H], F32) for t in range(PACK)]
         st_rounded = sb("st_rounded", [P, PACK, H], BF16)
+        z2_rows = sb("z2_rows", [P, PACK, N], BF16)
+        z2_grouped = sb("z2_grouped", [P, N, PACK], BF16)
 
         def fetch_n1(t):
-            for lo, hi in halves:
-                nc.vector.tensor_copy(a_n1[t][:, lo:hi], a_rows[t][:].indirect(entries(n1_l, lo, hi)))
+            nc.vector.tensor_copy(st_win[t][:, H : 2 * H], a_win[t][:].indirect(n1_l[:]))
 
         def larger(t):
-            nc.vector.tensor_tensor(st_rows[t][:], a_rows[t][:], a_n1[t][:], ALU.max)
-            nc.scalar.copy(st_rounded[:, t, :], st_rows[t][:])
+            nc.vector.tensor_tensor(st_win[t][:, 0:H], a_win[t][:, 0:H], st_win[t][:, H : 2 * H], ALU.max)
+
+        def round_st(t):
+            nc.scalar.copy(st_rounded[:, t, :], st_win[t][:, 0:H])
 
         fetch_n1(0)
-        fetch_n1(1)
-        larger(0)
-        fetch_n1(2)
-        larger(1)
-        wb_codes, wb_scales = quantize_weight("wb", wb_grouped)
-        z2_rows = sb("z2_rows", [P, PACK, N], BF16)
+        for t in range(1, PACK):
+            fetch_n1(t)
+            larger(t - 1)
+        round_st(0)
+        round_st(1)
         for t in range(PACK):
             acc = bank(4 + t, "b_ps%d" % t)
             product(acc, xb_words, xb_scales, t, wb_codes, wb_scales)
             nc.scalar.activation(z2_rows[:, t, :], acc[:], ACT.Copy, scale=gi_signed[:, t : t + 1])
-        fetch_n1(3)
-        larger(2)
 
         z_grouped = sb("z_grouped", [P, PACK, P, PACK], BF16)
-        z_rows = [sb("z_rows%d" % i, [P, PACK, 256], BF16) for i in range(2)]
-        st_n2 = [sb("st_n2_0", [P, PACK, 256], BF16)]
-
-        def fetch_n2(i, t):
-            lo, hi = halves[i]
-            nc.vector.tensor_copy(st_n2[i][:, t, :], st_rows[t][:].indirect(entries(n2_l, lo, hi)))
-
-        def smaller(i, ts):
-            lo, hi = halves[i]
-            nc.vector.tensor_tensor(z_rows[i][:, ts, :], st_rounded[:, ts, lo:hi], st_n2[i][:, ts, :], ALU.min)
-
-        def deal_z(engine_copy, i, us):
-            lo, hi = halves[i]
-            engine_copy(
-                out=z_grouped[:, us, lo // 4 : hi // 4, :].rearrange("p u m t -> p m t u"),
-                in_=z_rows[i][:].rearrange("p t (m u) -> p m t u", u=4)[:, :, :, us],
-            )
-
-        fetch_n2(0, 0)
-        larger(3)
-        z2_grouped = sb("z2_grouped", [P, N, PACK], BF16)
-        interleave(nc.scalar.copy, z2_grouped[:], z2_rows[:])
-        st_n2.append(sb("st_n2_1", [P, PACK, 256], BF16, tag="a_n1_3"))
-        for t in range(1, PACK):
-            fetch_n2(0, t)
-        fetch_n2(1, 0)
-        smaller(0, slice(0, 4))
-        deal_z(nc.scalar.copy, 0, slice(0, 4))
-        for t in range(1, PACK):
-            fetch_n2(1, t)
+        z_rows = sb("z_rows", [P, PACK, H], BF16)
+        st_n2 = sb("st_n2", [P, PACK, H], BF16)
         z2_codes = sb("z2_codes", [P, N], U32)
         z2_scales = sb("z2_scales", [P, N], U8)
-        smaller(1, slice(0, 3))
-        smaller(1, slice(3, 4))
+
+        def fetch_n2(t):
+            nc.vector.tensor_copy(st_n2[:, t, :], st_win[t][:].indirect(n2_l[:]))
+
+        def smaller(ts):
+            nc.vector.tensor_tensor(z_rows[:, ts, :], st_rounded[:, ts, :], st_n2[:, ts, :], ALU.min)
+
+        def deal_z(engine_copy, us):
+            engine_copy(
+                out=z_grouped[:, us, :, :].rearrange("p u m t -> p m t u"),
+                in_=z_rows[:].rearrange("p t (m u) -> p m t u", u=4)[:, :, :, us],
+            )
+
+        fetch_n2(0)
+        larger(3)
+        round_st(2)
+        interleave(nc.scalar.copy, z2_grouped[:], z2_rows[:])
+        round_st(3)
+        for t in range(1, PACK):
+            fetch_n2(t)
+        smaller(slice(0, 3))
         quantize(z2_codes, z2_scales, z2_grouped[:].rearrange("p c t -> p (c t)"), 0, N)
-        deal_z(nc.vector.tensor_copy, 1, slice(0, 1))
-        deal_z(nc.scalar.copy, 1, slice(1, 4))
+        smaller(slice(3, 4))
+        deal_z(nc.vector.tensor_copy, slice(0, 1))
+        deal_z(nc.scalar.copy, slice(1, 2))
 
         z_codes = sb("z_codes", [P, H], U32)
         z_scales = sb("z_scales", [P, H], U8)
-        cv_rows = [sb("cv_rows%d" % u, [P, N], F32) for u in range(PACK)]
-        cv_part = [sb("cv_part%d" % u, [P, N], F32) for u in range(PACK)]
+        cv_win, part_win = a_win, st_win
 
         def quantize_z(u):
             quantize(z_codes, z_scales, z_grouped[:, u, :, :].rearrange("p m t -> p (m t)"), u * P, (u + 1) * P)
 
         quantize_z(0)
         first = [bank(0, "cv_ps0_lo"), bank(4, "cv_ps0_hi")]
-        for acc, (lo, hi) in zip(first, halves):
+        for acc, (lo, hi) in zip(first, HALVES):
             product(acc, z_codes, z_scales, 0, z2_codes, z2_scales, lo, hi)
-        nc.scalar.activation(cv_part[0][:, 0:256], first[0][:, 0:256], ACT.Copy, scale=0.75 * 0.0625)
-        for u in range(1, PACK):
-            quantize_z(u)
-        nc.vector.tensor_scalar(cv_part[0][:, 256:512], first[1][:, 0:256], 0.75 * 0.0625, None, ALU.mult)
-        for acc, (lo, hi) in zip(first, halves):
-            nc.scalar.activation(cv_rows[0][:, lo:hi], acc[:, 0:256], ACT.Copy, scale=0.0625)
+        nc.scalar.activation(part_win[0][:, 0:256], first[0][:, 0:256], ACT.Copy, scale=0.75 * 0.0625)
+        quantize_z(1)
+        nc.vector.tensor_scalar(part_win[0][:, 256:512], first[1][:, 0:256], 0.75 * 0.0625, None, ALU.mult)
+        for acc, (lo, hi) in zip(first, HALVES):
+            nc.scalar.activation(cv_win[0][:, lo:hi], acc[:, 0:256], ACT.Copy, scale=0.0625)
+        deal_z(nc.scalar.copy, slice(2, 4))
+        nc.vector.quantize_mx(
+            out=z_codes[:, 2 * P : 4 * P].bitcast(FP8X4),
+            scales=z_scales[:, 2 * P : 4 * P],
+            in_=z_grouped[:, 2:4, :, :].rearrange("p u m t -> p (u m t)"),
+        )
         for u in range(1, PACK):
             acc = bank(u, "cv_ps%d" % u)
             product(acc, z_codes, z_scales, u, z2_codes, z2_scales)
-            nc.scalar.activation(cv_part[u][:], acc[:], ACT.Copy, scale=0.75 * 0.0625)
-            nc.scalar.activation(cv_rows[u][:], acc[:], ACT.Copy, scale=0.0625)
+            nc.scalar.activation(part_win[u][:, 0:N], acc[:], ACT.Copy, scale=0.75 * 0.0625)
+            nc.scalar.activation(cv_win[u][:, 0:N], acc[:], ACT.Copy, scale=0.0625)
 
         out_codes = sb("out_codes", [P, N], U32)
         out_scales = sb("out_scales", [P, N], U8)
         out_view = out_0.rearrange("(p u) n -> p u n", u=PACK)
         words_view = out_1[0].rearrange("p c r -> p (c r)").bitcast(I32)
-        result = [sb("result%d" % i, [P, PACK, hi - lo], F32) for i, (lo, hi) in enumerate(PIECES)]
-        out_grouped = [sb("out_grouped%d" % i, [P, hi - lo, PACK], BF16) for i, (lo, hi) in enumerate(PIECES)]
+        result = sb("result", [P, PACK, N], F32)
+        out_grouped = [sb("out_grouped%d" % lo, [P, hi - lo, PACK], BF16) for lo, hi in PIECES]
+        cv_n4 = [sb("cv_n4_%d" % u, [P, N], F32) for u in range(PACK)]
+        prod3 = [sb("prod3_%d" % u, [P, N], F32) for u in range(PACK)]
+        prod45 = [sb("prod45_%d" % u, [P, N], F32) for u in range(PACK)]
 
-        def fetch_n4(dst, u, lo, hi):
-            nc.vector.tensor_copy(dst, cv_part[u][:].indirect(entries(n4_l, lo, hi)))
+        def products(u, lo, hi):
+            nc.vector.tensor_tensor(
+                prod3[u][:, lo:hi], cv_win[u][:].indirect(entries(n3_l, lo, hi)), part_win[u][:, lo:hi], ALU.mult
+            )
+            nc.vector.tensor_tensor(
+                prod45[u][:, lo:hi], cv_win[u][:].indirect(entries(n5_l, lo, hi)), cv_n4[u][:, lo:hi], ALU.mult
+            )
 
-        def times_n3(dst, u, lo, hi):
-            nc.vector.tensor_tensor(dst, cv_rows[u][:].indirect(entries(n3_l, lo, hi)), cv_part[u][:, lo:hi], ALU.mult)
-
-        def times_n5(dst, u, lo, hi, fetched):
-            nc.vector.tensor_tensor(dst, cv_rows[u][:].indirect(entries(n5_l, lo, hi)), fetched, ALU.mult)
-
-        def quantize_out(i, lo, hi):
-            start = PIECES[i][0]
-            quantize(out_codes, out_scales, out_grouped[i][:, lo - start : hi - start, :].rearrange("p c t -> p (c t)"), lo, hi)
-
-        lo, hi = PIECES[0]
-        for u in range(PACK):
-            cv_n4 = sb("cv_n4_%d" % u, [P, hi - lo], F32)
-            prod3 = sb("prod3_%d" % u, [P, hi - lo], F32)
-            prod45 = sb("prod45_%d" % u, [P, hi - lo], F32)
-            fetch_n4(cv_n4[:], u, lo, hi)
-            times_n3(prod3[:], u, lo, hi)
-            times_n5(prod45[:], u, lo, hi, cv_n4[:])
-            turned_ps = bank(4 + u % 2, "turned_ps%d" % u)
-            for b in range(3):
-                cols = slice(b * P, (b + 1) * P)
-                nc.tensor.matmul(turned_ps[:, cols], prod3[:, cols], ident[:], start=True, stop=False, is_transpose=True)
-                nc.tensor.matmul(turned_ps[:, cols], prod45[:, cols], ident[:], start=False, stop=True, is_transpose=True)
-            turned = sb("turned%d" % u, [P, hi - lo], F32)
-            nc.scalar.copy(turned[:], turned_ps[:, 0 : hi - lo])
-            back_ps = bank(6 + u % 2, "back_ps%d" % u)
-            for b in range(3):
+        def add_by_transposes(u, half):
+            lo, hi = HALVES[half]
+            turned_ps = bank(4 + half, "turned_ps%d_%d" % (u, half))
+            for b in range(2):
+                cols = slice(lo + b * P, lo + (b + 1) * P)
+                slot = turned_ps[:, b * P : (b + 1) * P]
+                nc.tensor.matmul(slot, prod3[u][:, cols], ident[:], start=True, stop=False, is_transpose=True)
+                nc.tensor.matmul(slot, prod45[u][:, cols], ident[:], start=False, stop=True, is_transpose=True)
+            turned = sb("turned%d_%d" % (u, half), [P, 256], F32)
+            nc.scalar.copy(turned[:], turned_ps[:, 0:256])
+            back_ps = bank(6 + half, "back_ps%d_%d" % (u, half))
+            for b in range(2):
                 cols = slice(b * P, (b + 1) * P)
                 nc.tensor.transpose(back_ps[:, cols], turned[:, cols], ident[:])
-            nc.scalar.copy(result[0][:, u, :], back_ps[:, 0 : hi - lo])
-            nc.sync.dma_start(out_view[:, u, lo:hi], result[0][:, u, :])
-        interleave(nc.scalar.copy, out_grouped[0][:, 0:256, :], result[0][:, :, 0:256])
-        interleave(nc.scalar.copy, out_grouped[0][:, 256:384, :], result[0][:, :, 256:384])
+            nc.scalar.copy(result[:, u, lo:hi], back_ps[:, 0:256])
 
-        lo, hi = PIECES[1]
-        last = sb("last", [P, 2, PACK, hi - lo], F32, tag="cv_n4_2")
-        last45 = sb("last45", [P, PACK, hi - lo], F32)
-        for u in range(PACK):
-            fetch_n4(last[:, 0, u, :], u, lo, hi)
-            times_n3(last[:, 1, u, :], u, lo, hi)
-        for u in range(PACK):
-            times_n5(last45[:, u, :], u, lo, hi, last[:, 0, u, :])
-        quantize_out(0, 0, 256)
-        nc.vector.tensor_tensor(result[1][:], last[:, 1, :, :], last45[:], ALU.add)
-        nc.sync.dma_start(out_view[:, :, lo:hi], result[1][:])
-        quantize_out(0, 256, 384)
-        nc.sync.dma_start(words_view[:, 0:384], out_codes[:, 0:384].bitcast(I32))
-        interleave(nc.vector.tensor_copy, out_grouped[1][:], result[1][:])
-        quantize_out(1, 384, 512)
-        nc.sync.dma_start(words_view[:, 384:512], out_codes[:, 384:512].bitcast(I32))
+        def add_last(i):
+            lo, hi = PIECES[i]
+            nc.vector.tensor_tensor(result[:, 3, lo:hi], prod3[3][:, lo:hi], prod45[3][:, lo:hi], ALU.add)
+            nc.sync.dma_start(out_view[:, 3, lo:hi], result[:, 3, lo:hi])
+
+        def round_out(engine_copy, i):
+            lo, hi = PIECES[i]
+            interleave(engine_copy, out_grouped[i][:], result[:, :, lo:hi])
+
+        def quantize_out(i):
+            lo, hi = PIECES[i]
+            quantize(out_codes, out_scales, out_grouped[i][:].rearrange("p c t -> p (c t)"), lo, hi)
+            nc.sync.dma_start(words_view[:, lo:hi], out_codes[:, lo:hi].bitcast(I32))
+
+        for u in range(PACK - 1):
+            nc.vector.tensor_copy(cv_n4[u][:], part_win[u][:].indirect(n4_l[:]))
+            if u < 2:
+                products(u, 0, N)
+            for half in range(2):
+                if u == 2:
+                    products(u, *HALVES[half])
+                add_by_transposes(u, half)
+            nc.sync.dma_start(out_view[:, u, :], result[:, u, :])
+        nc.vector.tensor_copy(cv_n4[3][:], part_win[3][:].indirect(n4_l[:]))
+        products(3, *PIECES[0])
+        products(3, *PIECES[1])
+        add_last(0)
+        round_out(nc.scalar.copy, 0)
+        add_last(1)
+        round_out(nc.scalar.copy, 1)
+        products(3, *PIECES[2])
+        quantize_out(0)
+        add_last(2)
+        quantize_out(1)
+        round_out(nc.vector.tensor_copy, 2)
+        quantize_out(2)
         for q in range(4):
             queue = nc.scalar if q % 2 == 0 else nc.sync
             queue.dma_start(

@@ -4,7 +4,7 @@ import concourse.mybir as mybir
 from concourse.masks import make_identity
 
 K, T, S, N, H = 512, 2048, 512, 512, 512
-FLOPS = 3 * 2 * 512 * 512 * 512
+FLOPS = 2 * K * S * H + 2 * K * S * N + 2 * S * H * N
 
 F32 = mybir.dt.float32
 BF16 = mybir.dt.bfloat16
@@ -18,8 +18,13 @@ ACT = mybir.ActivationFunctionType
 
 P = 128
 PACK = 4
-HALVES = ((0, 256), (256, 512))
+RUN = 8
+HALF = 256
+HALVES = ((0, HALF), (HALF, 2 * HALF))
+LAST = PACK - 1
 PIECES = ((0, 256), (256, 384), (384, 512))
+CV_SCALE = 0.0625
+PART_SCALE = 0.75 * CV_SCALE
 
 
 def entries(offsets, lo, hi):
@@ -59,8 +64,8 @@ def tile_picked_momhopmndot_none_po_kernel(
                 in_=grouped,
             )
 
-        def product(out, lhs_codes, lhs_scales, t, rhs_codes, rhs_scales, lo=0, hi=512):
-            cols = slice(t * P, (t + 1) * P)
+        def product(out, lhs_codes, lhs_scales, tile, rhs_codes, rhs_scales, lo=0, hi=512):
+            cols = slice(tile * P, (tile + 1) * P)
             nc.tensor.matmul_mx(
                 out=out[:, 0 : hi - lo],
                 lhsT=lhs_codes[:, cols].bitcast(FP8X4),
@@ -79,18 +84,20 @@ def tile_picked_momhopmndot_none_po_kernel(
             return raw
 
         scale_rows = sb("scale_rows", [P, T // 4], I32)
-        for q in range(4):
-            queue = nc.sync if q < 2 else nc.scalar
-            queue.dma_start(scale_rows[32 * q : 32 * q + 4, :], x_scales[0][4 * q : 4 * q + 4, :].bitcast(I32))
+        for quad in range(4):
+            queue = nc.sync if quad < 2 else nc.scalar
+            queue.dma_start(
+                scale_rows[32 * quad : 32 * quad + 4, :], x_scales[0][4 * quad : 4 * quad + 4, :].bitcast(I32)
+            )
         offs_l = load_list("offs_l", offs)
         gains = sb("gains", [P, P], F32)
-        nc.gpsimd.memset(gains[:], 0.0)
+        nc.gpsimd.memset(gains[0:64, :], 0.0)
         two_l = load_list("two_l", two)
-        wa_raw = [load_weight(a_win[0][:], wa, 0, 256), load_weight(a_win[1][:], wa, 256, 512)]
-        for row, g in ((0, gt), (4, gi)):
+        wa_raw = [load_weight(a_win[h][:], wa, lo, hi) for h, (lo, hi) in enumerate(HALVES)]
+        for row, gain in ((0, gt), (PACK, gi)):
             nc.sync.dma_start(
-                gains[row : row + 4, :].rearrange("t (q r) -> t q r", r=8),
-                g.rearrange("(q t r) o -> t q (r o)", t=4, r=8),
+                gains[row : row + PACK, :].rearrange("t (q r) -> t q r", r=RUN),
+                gain.rearrange("(q t r) o -> t q (r o)", t=PACK, r=RUN),
             )
         table_words = sb("table_words", [P, T], I32)
         nc.sync.dma_start(table_words[:], x_words[0].rearrange("p c r -> p (c r)").bitcast(I32))
@@ -104,12 +111,12 @@ def tile_picked_momhopmndot_none_po_kernel(
 
         table_scales = sb("table_scales", [P, T], U8)
         nc.vector.memset(table_scales[:].bitcast(I32), 0)
-        for q in range(4):
-            nc.vector.tensor_copy(table_scales[32 * q : 32 * q + 4, :].bitcast(I32), scale_rows[32 * q : 32 * q + 4, :])
+        for quad in range(4):
+            rows = slice(32 * quad, 32 * quad + 4)
+            nc.vector.tensor_copy(table_scales[rows, :].bitcast(I32), scale_rows[rows, :])
         ident = sb("ident", [P, P], F32)
         make_identity(nc, ident[:])
-        warm = sb("warm", [P, 1], F32)
-        nc.scalar.copy(warm[:], ident[:, 0:1])
+        nc.scalar.activation(gains[64:P, :], ident[64:P, :], ACT.Copy, scale=0.0)
 
         gains_ps = bank(7, "gains_ps")
         nc.tensor.transpose(gains_ps[:, 0:P], gains[:], ident[:])
@@ -125,21 +132,21 @@ def tile_picked_momhopmndot_none_po_kernel(
         def pick_words(name, offsets):
             words = sb(name, [P, S], U32)
             nc.vector.tensor_copy(
-                words[:].rearrange("p (t q r) -> p q t r", t=4, r=8),
+                words[:].rearrange("p (t q r) -> p q t r", t=PACK, r=RUN),
                 table_words[:].bitcast(U32).indirect(offsets[:]),
             )
             return words
 
         def pick_scales(name, offsets):
-            listed = sb(name + "_listed", [P, S], U8)
+            listed = sb(name, [P, S], U8)
             nc.vector.tensor_copy(listed[:], table_scales[:].indirect(offsets[:]))
             return listed
 
         def deal_scales(name, listed):
             scales = sb(name, [P, S], U8)
             nc.vector.tensor_copy(
-                scales[:].bitcast(I32).rearrange("p (t q w) -> p t q w", t=4, w=2),
-                listed[:].bitcast(I32).rearrange("p (q t w) -> p t q w", t=4, w=2),
+                scales[:].bitcast(I32).rearrange("p (t q w) -> p t q w", t=PACK, w=RUN // 4),
+                listed[:].bitcast(I32).rearrange("p (q t w) -> p t q w", t=PACK, w=RUN // 4),
             )
             return scales
 
@@ -147,15 +154,15 @@ def tile_picked_momhopmndot_none_po_kernel(
             lo, hi = HALVES[half]
             quantize(codes, scales, grouped[:].rearrange("p c t -> p (c t)"), lo, hi)
 
-        wa_grouped = [sb("wa_grouped%d" % h, [P, 256, PACK], BF16) for h in range(2)]
-        wb_grouped = [sb("wb_grouped%d" % h, [P, 256, PACK], BF16) for h in range(2)]
+        wa_grouped = [sb("wa_grouped%d" % h, [P, HALF, PACK], BF16) for h in range(2)]
+        wb_grouped = [sb("wb_grouped%d" % h, [P, HALF, PACK], BF16) for h in range(2)]
         wa_codes, wa_scales = sb("wa_codes", [P, H], U32), sb("wa_scales", [P, H], U8)
         wb_codes, wb_scales = sb("wb_codes", [P, N], U32), sb("wb_scales", [P, N], U8)
 
         for h in range(2):
             interleave(nc.scalar.copy, wa_grouped[h][:], wa_raw[h])
-        xa_listed = pick_scales("xa", offs_l)
-        xb_listed = pick_scales("xb", two_l)
+        xa_listed = pick_scales("xa_listed", offs_l)
+        xb_listed = pick_scales("xb_listed", two_l)
         xa_scales = deal_scales("xa_scales", xa_listed)
         for h in range(2):
             quantize_half(wa_codes, wa_scales, wa_grouped[h], h)
@@ -166,7 +173,7 @@ def tile_picked_momhopmndot_none_po_kernel(
         for number, (lo, hi) in zip((0, 4), HALVES):
             acc = bank(number, "a_ps0_%d" % lo)
             product(acc, xa_words, xa_scales, 0, wa_codes, wa_scales, lo, hi)
-            nc.scalar.activation(a_win[0][:, lo:hi], acc[:, 0:256], ACT.Copy, scale=gt_abs[:, 0:1])
+            nc.scalar.activation(a_win[0][:, lo:hi], acc[:, 0:HALF], ACT.Copy, scale=gt_abs[:, 0:1])
         for i in range(4):
             interleave(nc.scalar.copy, wb_grouped[i // 2][:, P * (i % 2) : P * (i % 2 + 1), :], wb_raw[i])
         for h in range(2):
@@ -196,6 +203,7 @@ def tile_picked_momhopmndot_none_po_kernel(
             larger(t - 1)
         round_st(0)
         round_st(1)
+
         for t in range(PACK):
             acc = bank(4 + t, "b_ps%d" % t)
             product(acc, xb_words, xb_scales, t, wb_codes, wb_scales)
@@ -203,7 +211,7 @@ def tile_picked_momhopmndot_none_po_kernel(
 
         z_grouped = sb("z_grouped", [P, PACK, P, PACK], BF16)
         z_rows = sb("z_rows", [P, PACK, H], BF16)
-        st_n2 = sb("st_n2", [P, PACK, H], BF16)
+        st_n2 = sb("st_n2", [P, PACK, H], BF16, tag="wb_grouped1")
         z2_codes = sb("z2_codes", [P, N], U32)
         z2_scales = sb("z2_scales", [P, N], U8)
 
@@ -216,19 +224,19 @@ def tile_picked_momhopmndot_none_po_kernel(
         def deal_z(engine_copy, us):
             engine_copy(
                 out=z_grouped[:, us, :, :].rearrange("p u m t -> p m t u"),
-                in_=z_rows[:].rearrange("p t (m u) -> p m t u", u=4)[:, :, :, us],
+                in_=z_rows[:].rearrange("p t (m u) -> p m t u", u=PACK)[:, :, :, us],
             )
 
         fetch_n2(0)
-        larger(3)
-        round_st(2)
+        larger(LAST)
         interleave(nc.scalar.copy, z2_grouped[:], z2_rows[:])
-        round_st(3)
+        round_st(2)
+        round_st(LAST)
         for t in range(1, PACK):
             fetch_n2(t)
-        smaller(slice(0, 3))
         quantize(z2_codes, z2_scales, z2_grouped[:].rearrange("p c t -> p (c t)"), 0, N)
-        smaller(slice(3, 4))
+        smaller(slice(0, LAST))
+        smaller(slice(LAST, PACK))
         deal_z(nc.vector.tensor_copy, slice(0, 1))
         deal_z(nc.scalar.copy, slice(1, 2))
 
@@ -236,29 +244,26 @@ def tile_picked_momhopmndot_none_po_kernel(
         z_scales = sb("z_scales", [P, H], U8)
         cv_win, part_win = a_win, st_win
 
-        def quantize_z(u):
-            quantize(z_codes, z_scales, z_grouped[:, u, :, :].rearrange("p m t -> p (m t)"), u * P, (u + 1) * P)
+        def quantize_z(first, last):
+            grouped = z_grouped[:, first:last, :, :].rearrange("p u m t -> p (u m t)")
+            quantize(z_codes, z_scales, grouped, first * P, last * P)
 
-        quantize_z(0)
-        first = [bank(0, "cv_ps0_lo"), bank(4, "cv_ps0_hi")]
-        for acc, (lo, hi) in zip(first, HALVES):
+        quantize_z(0, 1)
+        cv0_ps = [bank(0, "cv_ps0_lo"), bank(4, "cv_ps0_hi")]
+        for acc, (lo, hi) in zip(cv0_ps, HALVES):
             product(acc, z_codes, z_scales, 0, z2_codes, z2_scales, lo, hi)
-        nc.scalar.activation(part_win[0][:, 0:256], first[0][:, 0:256], ACT.Copy, scale=0.75 * 0.0625)
-        quantize_z(1)
-        nc.vector.tensor_scalar(part_win[0][:, 256:512], first[1][:, 0:256], 0.75 * 0.0625, None, ALU.mult)
-        for acc, (lo, hi) in zip(first, HALVES):
-            nc.scalar.activation(cv_win[0][:, lo:hi], acc[:, 0:256], ACT.Copy, scale=0.0625)
-        deal_z(nc.scalar.copy, slice(2, 4))
-        nc.vector.quantize_mx(
-            out=z_codes[:, 2 * P : 4 * P].bitcast(FP8X4),
-            scales=z_scales[:, 2 * P : 4 * P],
-            in_=z_grouped[:, 2:4, :, :].rearrange("p u m t -> p (u m t)"),
-        )
+        nc.scalar.activation(part_win[0][:, 0:HALF], cv0_ps[0][:, 0:HALF], ACT.Copy, scale=PART_SCALE)
+        quantize_z(1, 2)
+        nc.vector.tensor_scalar(part_win[0][:, HALF:N], cv0_ps[1][:, 0:HALF], PART_SCALE, None, ALU.mult)
+        for acc, (lo, hi) in zip(cv0_ps, HALVES):
+            nc.scalar.activation(cv_win[0][:, lo:hi], acc[:, 0:HALF], ACT.Copy, scale=CV_SCALE)
+        deal_z(nc.scalar.copy, slice(2, PACK))
+        quantize_z(2, PACK)
         for u in range(1, PACK):
             acc = bank(u, "cv_ps%d" % u)
             product(acc, z_codes, z_scales, u, z2_codes, z2_scales)
-            nc.scalar.activation(part_win[u][:, 0:N], acc[:], ACT.Copy, scale=0.75 * 0.0625)
-            nc.scalar.activation(cv_win[u][:, 0:N], acc[:], ACT.Copy, scale=0.0625)
+            nc.scalar.activation(part_win[u][:, 0:N], acc[:], ACT.Copy, scale=PART_SCALE)
+            nc.scalar.activation(cv_win[u][:, 0:N], acc[:], ACT.Copy, scale=CV_SCALE)
 
         out_codes = sb("out_codes", [P, N], U32)
         out_scales = sb("out_scales", [P, N], U8)
@@ -266,73 +271,82 @@ def tile_picked_momhopmndot_none_po_kernel(
         words_view = out_1[0].rearrange("p c r -> p (c r)").bitcast(I32)
         result = sb("result", [P, PACK, N], F32)
         out_grouped = [sb("out_grouped%d" % lo, [P, hi - lo, PACK], BF16) for lo, hi in PIECES]
-        cv_n4 = [sb("cv_n4_%d" % u, [P, N], F32) for u in range(PACK)]
+        part_n4 = [sb("part_n4_%d" % u, [P, N], F32) for u in range(PACK)]
         prod3 = [sb("prod3_%d" % u, [P, N], F32) for u in range(PACK)]
         prod45 = [sb("prod45_%d" % u, [P, N], F32) for u in range(PACK)]
 
-        def products(u, lo, hi):
+        def fetch_n4(u):
+            nc.vector.tensor_copy(part_n4[u][:], part_win[u][:].indirect(n4_l[:]))
+
+        def times_n3(u, lo, hi):
             nc.vector.tensor_tensor(
                 prod3[u][:, lo:hi], cv_win[u][:].indirect(entries(n3_l, lo, hi)), part_win[u][:, lo:hi], ALU.mult
             )
+
+        def times_n5(u, lo, hi):
             nc.vector.tensor_tensor(
-                prod45[u][:, lo:hi], cv_win[u][:].indirect(entries(n5_l, lo, hi)), cv_n4[u][:, lo:hi], ALU.mult
+                prod45[u][:, lo:hi], cv_win[u][:].indirect(entries(n5_l, lo, hi)), part_n4[u][:, lo:hi], ALU.mult
             )
 
         def add_by_transposes(u, half):
             lo, hi = HALVES[half]
             turned_ps = bank(4 + half, "turned_ps%d_%d" % (u, half))
-            for b in range(2):
-                cols = slice(lo + b * P, lo + (b + 1) * P)
-                slot = turned_ps[:, b * P : (b + 1) * P]
+            for block in range(HALF // P):
+                cols = slice(lo + block * P, lo + (block + 1) * P)
+                slot = turned_ps[:, block * P : (block + 1) * P]
                 nc.tensor.matmul(slot, prod3[u][:, cols], ident[:], start=True, stop=False, is_transpose=True)
                 nc.tensor.matmul(slot, prod45[u][:, cols], ident[:], start=False, stop=True, is_transpose=True)
-            turned = sb("turned%d_%d" % (u, half), [P, 256], F32)
-            nc.scalar.copy(turned[:], turned_ps[:, 0:256])
+            turned = sb("turned%d_%d" % (u, half), [P, HALF], F32)
+            nc.scalar.copy(turned[:], turned_ps[:, 0:HALF])
             back_ps = bank(6 + half, "back_ps%d_%d" % (u, half))
-            for b in range(2):
-                cols = slice(b * P, (b + 1) * P)
+            for block in range(HALF // P):
+                cols = slice(block * P, (block + 1) * P)
                 nc.tensor.transpose(back_ps[:, cols], turned[:, cols], ident[:])
-            nc.scalar.copy(result[:, u, lo:hi], back_ps[:, 0:256])
+            nc.scalar.copy(result[:, u, lo:hi], back_ps[:, 0:HALF])
 
-        def add_last(i):
-            lo, hi = PIECES[i]
-            nc.vector.tensor_tensor(result[:, 3, lo:hi], prod3[3][:, lo:hi], prod45[3][:, lo:hi], ALU.add)
-            nc.sync.dma_start(out_view[:, 3, lo:hi], result[:, 3, lo:hi])
+        def add_last(piece):
+            lo, hi = PIECES[piece]
+            nc.vector.tensor_tensor(result[:, LAST, lo:hi], prod3[LAST][:, lo:hi], prod45[LAST][:, lo:hi], ALU.add)
+            nc.sync.dma_start(out_view[:, LAST, lo:hi], result[:, LAST, lo:hi])
 
-        def round_out(engine_copy, i):
-            lo, hi = PIECES[i]
-            interleave(engine_copy, out_grouped[i][:], result[:, :, lo:hi])
+        def round_out(engine_copy, piece):
+            lo, hi = PIECES[piece]
+            interleave(engine_copy, out_grouped[piece][:], result[:, :, lo:hi])
 
-        def quantize_out(i):
-            lo, hi = PIECES[i]
-            quantize(out_codes, out_scales, out_grouped[i][:].rearrange("p c t -> p (c t)"), lo, hi)
+        def quantize_out(piece):
+            lo, hi = PIECES[piece]
+            quantize(out_codes, out_scales, out_grouped[piece][:].rearrange("p c t -> p (c t)"), lo, hi)
             nc.sync.dma_start(words_view[:, lo:hi], out_codes[:, lo:hi].bitcast(I32))
 
-        for u in range(PACK - 1):
-            nc.vector.tensor_copy(cv_n4[u][:], part_win[u][:].indirect(n4_l[:]))
-            if u < 2:
-                products(u, 0, N)
-            for half in range(2):
-                if u == 2:
-                    products(u, *HALVES[half])
-                add_by_transposes(u, half)
+        for u in range(LAST):
+            fetch_n4(u)
+            spans = HALVES if u == LAST - 1 else ((0, N),)
+            for lo, hi in spans:
+                times_n3(u, lo, hi)
+                times_n5(u, lo, hi)
+                for half in range(lo // HALF, hi // HALF):
+                    add_by_transposes(u, half)
             nc.sync.dma_start(out_view[:, u, :], result[:, u, :])
-        nc.vector.tensor_copy(cv_n4[3][:], part_win[3][:].indirect(n4_l[:]))
-        products(3, *PIECES[0])
-        products(3, *PIECES[1])
+
+        fetch_n4(LAST)
+        times_n3(LAST, *PIECES[0])
+        times_n5(LAST, *PIECES[0])
+        times_n3(LAST, *PIECES[1])
         add_last(0)
         round_out(nc.scalar.copy, 0)
+        times_n5(LAST, *PIECES[1])
+        times_n3(LAST, *PIECES[2])
         add_last(1)
         round_out(nc.scalar.copy, 1)
-        products(3, *PIECES[2])
+        times_n5(LAST, *PIECES[2])
         quantize_out(0)
         add_last(2)
         quantize_out(1)
         round_out(nc.vector.tensor_copy, 2)
         quantize_out(2)
-        for q in range(4):
-            queue = nc.scalar if q % 2 == 0 else nc.sync
+        for quad in range(4):
+            queue = nc.scalar if quad % 2 == 0 else nc.sync
             queue.dma_start(
-                out_2[0][4 * q : 4 * q + 4, :].bitcast(I32),
-                out_scales[32 * q : 32 * q + 4, :].bitcast(I32),
+                out_2[0][4 * quad : 4 * quad + 4, :].bitcast(I32),
+                out_scales[32 * quad : 32 * quad + 4, :].bitcast(I32),
             )

from contextlib import ExitStack

import concourse.mybir as mybir
from concourse.masks import make_identity

K, T, S, N, H = 512, 2048, 512, 512, 512
FLOPS = 2 * K * S * H + 2 * K * S * N + 2 * S * H * N

F32 = mybir.dt.float32
BF16 = mybir.dt.bfloat16
I32 = mybir.dt.int32
U32 = mybir.dt.uint32
U16 = mybir.dt.uint16
U8 = mybir.dt.uint8
FP8X4 = mybir.dt.float8_e4m3fn_x4
ALU = mybir.AluOpType
ACT = mybir.ActivationFunctionType

P = 128
PACK = 4
RUN = 8
HALF = 256
HALVES = ((0, HALF), (HALF, 2 * HALF))
LAST = PACK - 1
PIECES = ((0, 256), (256, 384), (384, 512))
CV_SCALE = 0.0625
PART_SCALE = 0.75 * CV_SCALE


def entries(offsets, lo, hi):
    return offsets[:, lo // 16 : hi // 16]


def interleave(engine_copy, dst, src):
    engine_copy(
        out=dst.rearrange("p (c i) t -> p c t i", i=4),
        in_=src.rearrange("p t (c i) -> p c t i", i=4),
    )


def tile_picked_momhopmndot_none_po_kernel(
    tc, x_words, x_scales, wa, wb, gt, gi, offs, two, n1, n2, n3, n4, n5, out_0, out_1, out_2
):
    nc = tc.nc
    with ExitStack() as ctx:
        keep = ctx.enter_context(tc.tile_pool(name="keep", bufs=1))
        psum = ctx.enter_context(tc.psum_pool(name="psum", bufs=1))

        def sb(name, shape, dtype, tag=None):
            return keep.tile(shape, dtype, name=name, tag=tag or name, align_bytes=64)

        def bank(number, name):
            return psum.tile([P, 512], F32, name=name, tag="bank%d" % number)

        def load_list(name, source):
            tile = sb(name, [P, S // 16], U16)
            nc.sync.dma_start(tile[:], source)
            return tile

        def quantize(codes, scales, grouped, lo, hi):
            nc.vector.quantize_mx(
                out=codes[:, lo:hi].bitcast(FP8X4),
                scales=scales[:, lo:hi],
                in_=grouped,
            )

        def product(out, lhs_codes, lhs_scales, tile, rhs_codes, rhs_scales, lo=0, hi=512):
            cols = slice(tile * P, (tile + 1) * P)
            nc.tensor.matmul_mx(
                out=out[:, 0 : hi - lo],
                lhsT=lhs_codes[:, cols].bitcast(FP8X4),
                lhsT_scale=lhs_scales[:, cols],
                rhs=rhs_codes[:, lo:hi].bitcast(FP8X4),
                rhs_scale=rhs_scales[:, lo:hi],
                start=True,
                stop=True,
            )

        a_win = [sb("a_win%d" % t, [P, 2 * H], F32) for t in range(PACK)]

        def load_weight(space, w, lo, hi):
            raw = space.rearrange("p (j c) -> p j c", j=PACK)
            nc.sync.dma_start(raw, w.rearrange("(p j) c -> p j c", j=PACK)[:, :, lo:hi])
            return raw

        scale_rows = sb("scale_rows", [P, T // 4], I32)
        for quad in range(4):
            queue = nc.sync if quad < 2 else nc.scalar
            queue.dma_start(
                scale_rows[32 * quad : 32 * quad + 4, :], x_scales[0][4 * quad : 4 * quad + 4, :].bitcast(I32)
            )
        offs_l = load_list("offs_l", offs)
        gains = sb("gains", [P, P], F32)
        nc.gpsimd.memset(gains[0:64, :], 0.0)
        two_l = load_list("two_l", two)
        wa_raw = [load_weight(a_win[h][:], wa, lo, hi) for h, (lo, hi) in enumerate(HALVES)]
        for row, gain in ((0, gt), (PACK, gi)):
            nc.sync.dma_start(
                gains[row : row + PACK, :].rearrange("t (q r) -> t q r", r=RUN),
                gain.rearrange("(q t r) o -> t q (r o)", t=PACK, r=RUN),
            )
        table_words = sb("table_words", [P, T], I32)
        nc.sync.dma_start(table_words[:], x_words[0].rearrange("p c r -> p (c r)").bitcast(I32))
        n1_l = load_list("n1_l", n1)
        wb_space = [a_win[2][:, H : 2 * H], a_win[3][:, H : 2 * H], a_win[2][:, 0:H], a_win[3][:, 0:H]]
        wb_raw = [load_weight(wb_space[i], wb, P * i, P * (i + 1)) for i in range(4)]
        n2_l = load_list("n2_l", n2)
        n4_l = load_list("n4_l", n4)
        n3_l = load_list("n3_l", n3)
        n5_l = load_list("n5_l", n5)

        table_scales = sb("table_scales", [P, T], U8)
        nc.vector.memset(table_scales[:].bitcast(I32), 0)
        for quad in range(4):
            rows = slice(32 * quad, 32 * quad + 4)
            nc.vector.tensor_copy(table_scales[rows, :].bitcast(I32), scale_rows[rows, :])
        ident = sb("ident", [P, P], F32)
        make_identity(nc, ident[:])
        nc.scalar.activation(gains[64:P, :], ident[64:P, :], ACT.Copy, scale=0.0)

        gains_ps = bank(7, "gains_ps")
        nc.tensor.transpose(gains_ps[:, 0:P], gains[:], ident[:])
        gt_abs = sb("gt_abs", [P, PACK], F32)
        gt_sign = sb("gt_sign", [P, PACK], F32)
        gi_cols = sb("gi_cols", [P, PACK], F32)
        gi_signed = sb("gi_signed", [P, PACK], F32)
        nc.scalar.activation(gt_abs[:], gains_ps[:, 0:PACK], ACT.Abs)
        nc.scalar.activation(gt_sign[:], gains_ps[:, 0:PACK], ACT.Sign)
        nc.scalar.copy(gi_cols[:], gains_ps[:, PACK : 2 * PACK])
        nc.gpsimd.tensor_tensor(gi_signed[:], gi_cols[:], gt_sign[:], ALU.mult)

        def pick_words(name, offsets):
            words = sb(name, [P, S], U32)
            nc.vector.tensor_copy(
                words[:].rearrange("p (t q r) -> p q t r", t=PACK, r=RUN),
                table_words[:].bitcast(U32).indirect(offsets[:]),
            )
            return words

        def pick_scales(name, offsets):
            listed = sb(name, [P, S], U8)
            nc.vector.tensor_copy(listed[:], table_scales[:].indirect(offsets[:]))
            return listed

        def deal_scales(name, listed):
            scales = sb(name, [P, S], U8)
            nc.vector.tensor_copy(
                scales[:].bitcast(I32).rearrange("p (t q w) -> p t q w", t=PACK, w=RUN // 4),
                listed[:].bitcast(I32).rearrange("p (q t w) -> p t q w", t=PACK, w=RUN // 4),
            )
            return scales

        def quantize_half(codes, scales, grouped, half):
            lo, hi = HALVES[half]
            quantize(codes, scales, grouped[:].rearrange("p c t -> p (c t)"), lo, hi)

        wa_grouped = [sb("wa_grouped%d" % h, [P, HALF, PACK], BF16) for h in range(2)]
        wb_grouped = [sb("wb_grouped%d" % h, [P, HALF, PACK], BF16) for h in range(2)]
        wa_codes, wa_scales = sb("wa_codes", [P, H], U32), sb("wa_scales", [P, H], U8)
        wb_codes, wb_scales = sb("wb_codes", [P, N], U32), sb("wb_scales", [P, N], U8)

        for h in range(2):
            interleave(nc.scalar.copy, wa_grouped[h][:], wa_raw[h])
        xa_listed = pick_scales("xa_listed", offs_l)
        xb_listed = pick_scales("xb_listed", two_l)
        xa_scales = deal_scales("xa_scales", xa_listed)
        for h in range(2):
            quantize_half(wa_codes, wa_scales, wa_grouped[h], h)
        xb_scales = deal_scales("xb_scales", xb_listed)
        xa_words = pick_words("xa_words", offs_l)
        xb_words = pick_words("xb_words", two_l)

        for number, (lo, hi) in zip((0, 4), HALVES):
            acc = bank(number, "a_ps0_%d" % lo)
            product(acc, xa_words, xa_scales, 0, wa_codes, wa_scales, lo, hi)
            nc.scalar.activation(a_win[0][:, lo:hi], acc[:, 0:HALF], ACT.Copy, scale=gt_abs[:, 0:1])
        for i in range(4):
            interleave(nc.scalar.copy, wb_grouped[i // 2][:, P * (i % 2) : P * (i % 2 + 1), :], wb_raw[i])
        for h in range(2):
            quantize_half(wb_codes, wb_scales, wb_grouped[h], h)
        for t in range(1, PACK):
            acc = bank(t, "a_ps%d" % t)
            product(acc, xa_words, xa_scales, t, wa_codes, wa_scales)
            nc.scalar.activation(a_win[t][:, 0:H], acc[:], ACT.Copy, scale=gt_abs[:, t : t + 1])

        st_win = [sb("st_win%d" % t, [P, 2 * H], F32) for t in range(PACK)]
        st_rounded = sb("st_rounded", [P, PACK, H], BF16)
        z2_rows = sb("z2_rows", [P, PACK, N], BF16)
        z2_grouped = sb("z2_grouped", [P, N, PACK], BF16)

        def fetch_n1(t):
            nc.vector.tensor_copy(st_win[t][:, H : 2 * H], a_win[t][:].indirect(n1_l[:]))

        def larger(t):
            nc.vector.tensor_tensor(st_win[t][:, 0:H], a_win[t][:, 0:H], st_win[t][:, H : 2 * H], ALU.max)

        def round_st(t):
            nc.scalar.copy(st_rounded[:, t, :], st_win[t][:, 0:H])

        fetch_n1(0)
        for t in range(1, PACK):
            fetch_n1(t)
            larger(t - 1)
        round_st(0)
        round_st(1)

        for t in range(PACK):
            acc = bank(4 + t, "b_ps%d" % t)
            product(acc, xb_words, xb_scales, t, wb_codes, wb_scales)
            nc.scalar.activation(z2_rows[:, t, :], acc[:], ACT.Copy, scale=gi_signed[:, t : t + 1])

        z_grouped = sb("z_grouped", [P, PACK, P, PACK], BF16)
        z_rows = sb("z_rows", [P, PACK, H], BF16)
        st_n2 = sb("st_n2", [P, PACK, H], BF16, tag="wb_grouped1")
        z2_codes = sb("z2_codes", [P, N], U32)
        z2_scales = sb("z2_scales", [P, N], U8)

        def fetch_n2(t):
            nc.vector.tensor_copy(st_n2[:, t, :], st_win[t][:].indirect(n2_l[:]))

        def smaller(ts):
            nc.vector.tensor_tensor(z_rows[:, ts, :], st_rounded[:, ts, :], st_n2[:, ts, :], ALU.min)

        def deal_z(engine_copy, us):
            engine_copy(
                out=z_grouped[:, us, :, :].rearrange("p u m t -> p m t u"),
                in_=z_rows[:].rearrange("p t (m u) -> p m t u", u=PACK)[:, :, :, us],
            )

        fetch_n2(0)
        larger(LAST)
        interleave(nc.scalar.copy, z2_grouped[:], z2_rows[:])
        round_st(2)
        round_st(LAST)
        for t in range(1, PACK):
            fetch_n2(t)
        quantize(z2_codes, z2_scales, z2_grouped[:].rearrange("p c t -> p (c t)"), 0, N)
        smaller(slice(0, LAST))
        smaller(slice(LAST, PACK))
        deal_z(nc.vector.tensor_copy, slice(0, 1))
        deal_z(nc.scalar.copy, slice(1, 2))

        z_codes = sb("z_codes", [P, H], U32)
        z_scales = sb("z_scales", [P, H], U8)
        cv_win, part_win = a_win, st_win

        def quantize_z(first, last):
            grouped = z_grouped[:, first:last, :, :].rearrange("p u m t -> p (u m t)")
            quantize(z_codes, z_scales, grouped, first * P, last * P)

        quantize_z(0, 1)
        cv0_ps = [bank(0, "cv_ps0_lo"), bank(4, "cv_ps0_hi")]
        for acc, (lo, hi) in zip(cv0_ps, HALVES):
            product(acc, z_codes, z_scales, 0, z2_codes, z2_scales, lo, hi)
        nc.scalar.activation(part_win[0][:, 0:HALF], cv0_ps[0][:, 0:HALF], ACT.Copy, scale=PART_SCALE)
        quantize_z(1, 2)
        nc.vector.tensor_scalar(part_win[0][:, HALF:N], cv0_ps[1][:, 0:HALF], PART_SCALE, None, ALU.mult)
        for acc, (lo, hi) in zip(cv0_ps, HALVES):
            nc.scalar.activation(cv_win[0][:, lo:hi], acc[:, 0:HALF], ACT.Copy, scale=CV_SCALE)
        deal_z(nc.scalar.copy, slice(2, PACK))
        quantize_z(2, PACK)
        for u in range(1, PACK):
            acc = bank(u, "cv_ps%d" % u)
            product(acc, z_codes, z_scales, u, z2_codes, z2_scales)
            nc.scalar.activation(part_win[u][:, 0:N], acc[:], ACT.Copy, scale=PART_SCALE)
            nc.scalar.activation(cv_win[u][:, 0:N], acc[:], ACT.Copy, scale=CV_SCALE)

        out_codes = sb("out_codes", [P, N], U32)
        out_scales = sb("out_scales", [P, N], U8)
        out_view = out_0.rearrange("(p u) n -> p u n", u=PACK)
        words_view = out_1[0].rearrange("p c r -> p (c r)").bitcast(I32)
        result = sb("result", [P, PACK, N], F32)
        out_grouped = [sb("out_grouped%d" % lo, [P, hi - lo, PACK], BF16) for lo, hi in PIECES]
        part_n4 = [sb("part_n4_%d" % u, [P, N], F32) for u in range(PACK)]
        prod3 = [sb("prod3_%d" % u, [P, N], F32) for u in range(PACK)]
        prod45 = [sb("prod45_%d" % u, [P, N], F32) for u in range(PACK)]

        def fetch_n4(u):
            nc.vector.tensor_copy(part_n4[u][:], part_win[u][:].indirect(n4_l[:]))

        def times_n3(u, lo, hi):
            nc.vector.tensor_tensor(
                prod3[u][:, lo:hi], cv_win[u][:].indirect(entries(n3_l, lo, hi)), part_win[u][:, lo:hi], ALU.mult
            )

        def times_n5(u, lo, hi):
            nc.vector.tensor_tensor(
                prod45[u][:, lo:hi], cv_win[u][:].indirect(entries(n5_l, lo, hi)), part_n4[u][:, lo:hi], ALU.mult
            )

        def add_by_transposes(u, half):
            lo, hi = HALVES[half]
            turned_ps = bank(4 + half, "turned_ps%d_%d" % (u, half))
            for block in range(HALF // P):
                cols = slice(lo + block * P, lo + (block + 1) * P)
                slot = turned_ps[:, block * P : (block + 1) * P]
                nc.tensor.matmul(slot, prod3[u][:, cols], ident[:], start=True, stop=False, is_transpose=True)
                nc.tensor.matmul(slot, prod45[u][:, cols], ident[:], start=False, stop=True, is_transpose=True)
            turned = sb("turned%d_%d" % (u, half), [P, HALF], F32)
            nc.scalar.copy(turned[:], turned_ps[:, 0:HALF])
            back_ps = bank(6 + half, "back_ps%d_%d" % (u, half))
            for block in range(HALF // P):
                cols = slice(block * P, (block + 1) * P)
                nc.tensor.transpose(back_ps[:, cols], turned[:, cols], ident[:])
            nc.scalar.copy(result[:, u, lo:hi], back_ps[:, 0:HALF])

        def add_last(piece):
            lo, hi = PIECES[piece]
            nc.vector.tensor_tensor(result[:, LAST, lo:hi], prod3[LAST][:, lo:hi], prod45[LAST][:, lo:hi], ALU.add)
            nc.sync.dma_start(out_view[:, LAST, lo:hi], result[:, LAST, lo:hi])

        def round_out(engine_copy, piece):
            lo, hi = PIECES[piece]
            interleave(engine_copy, out_grouped[piece][:], result[:, :, lo:hi])

        def quantize_out(piece):
            lo, hi = PIECES[piece]
            quantize(out_codes, out_scales, out_grouped[piece][:].rearrange("p c t -> p (c t)"), lo, hi)
            nc.sync.dma_start(words_view[:, lo:hi], out_codes[:, lo:hi].bitcast(I32))

        for u in range(LAST):
            fetch_n4(u)
            spans = HALVES if u == LAST - 1 else ((0, N),)
            for lo, hi in spans:
                times_n3(u, lo, hi)
                times_n5(u, lo, hi)
                for half in range(lo // HALF, hi // HALF):
                    add_by_transposes(u, half)
            nc.sync.dma_start(out_view[:, u, :], result[:, u, :])

        fetch_n4(LAST)
        times_n3(LAST, *PIECES[0])
        times_n5(LAST, *PIECES[0])
        times_n3(LAST, *PIECES[1])
        add_last(0)
        round_out(nc.scalar.copy, 0)
        times_n5(LAST, *PIECES[1])
        times_n3(LAST, *PIECES[2])
        add_last(1)
        round_out(nc.scalar.copy, 1)
        times_n5(LAST, *PIECES[2])
        quantize_out(0)
        add_last(2)
        quantize_out(1)
        round_out(nc.vector.tensor_copy, 2)
        quantize_out(2)
        for quad in range(4):
            queue = nc.scalar if quad % 2 == 0 else nc.sync
            queue.dma_start(
                out_2[0][4 * quad : 4 * quad + 4, :].bitcast(I32),
                out_scales[32 * quad : 32 * quad + 4, :].bitcast(I32),
            )
